import numpy as np, ml_dtypes
CORES = [48,51,52,55]
N = 4
BF = ml_dtypes.bfloat16
def gentries(a):
    return np.ascontiguousarray(a.reshape(8, 16, -1).transpose(0, 2, 1)).reshape(8, -1)
def gtable(e):
    e = np.asarray(e); return np.ascontiguousarray(e.reshape(8, -1, 16).transpose(0, 2, 1)).reshape(128, -1).astype(np.int32)
V, R, L, T, M = 2048, 4096, 256, 8, 2048
def parts(rng):
    rec = rng.integers(0, 256, (N, 8, 16, R)); ch = rng.integers(0, R, (N, 8, 16, V)); at = rng.integers(0, 256, (N, 8, 16, L))
    key0 = np.where(rng.random((N, 8, L)) < 0.25, rng.integers(0, V // 16, (N, 8, L)), rng.integers(0, V, (N, 8, L)))
    th = rng.integers(1650, 2000, (N, 8, 1, 1)) + rng.integers(0, 250, (N, 8, 16, 1)); w = rng.integers(0, 16, (N, 8, 16, 1))
    return rec, ch, at, key0, th, w
def pack(rec, ch, at, key0, th, w):
    return {"rec": np.ascontiguousarray(rec.reshape(N, 128, R)).astype(np.float32).astype(BF), "ch": np.ascontiguousarray(ch.reshape(N, 128, V)).astype(np.int32),
            "at": np.ascontiguousarray(at.reshape(N, 128, L)).astype(np.float32).astype(BF), "key0": np.stack([gtable(a) for a in key0]),
            "th": np.ascontiguousarray(th.reshape(N, 128, 1)).astype(np.int32), "w": np.ascontiguousarray(w.reshape(N, 128, 1)).astype(np.int32)}
def setup_inputs(rng):
    return pack(*parts(rng))
def setup_inputs_clash(rng):
    rec, ch, at, key0, th, w = parts(rng); o = rng.permutation(L)
    at[..., o[1::2]] = at[..., o[0::2]]
    key0[:, 1::2] = rng.integers(0, V, (N, 4, 8))[np.arange(N)[:, None, None], np.arange(4)[None, :, None], rng.integers(0, 8, (N, 4, L))]
    key0[:, ::2, o[1::2]] = key0[:, ::2, o[0::2]]
    one = (np.arange(16)[None, None, :, None] == rng.integers(0, 16, (N, 8, 1, 1))).astype(np.int64)
    w = np.where((rng.random((N, 8, 1, 1)) < 0.5), one, w)
    w[rng.integers(0, N - 1), rng.integers(0, 8)] = 0
    ga, gb, gc = [int(i) for i in rng.permutation(8)[:3]]
    th[0, ga] = 4080; w[0, ga] = 0; th[1, ga] = 0
    for g in (gb, gc):
        key0[:, g] = np.argsort(rng.random((N, V)), axis=1)[:, :L]; th[0, g] = 0
    key0[:, gc, L - 1] = key0[:, gc, 0]
    return pack(rec, ch, at, key0, th, w)
def setup_inputs_ends(rng):
    rec, ch, at, key0, th, w = parts(rng)
    rec = 255 * (rng.random((N, 8, 16, R)) < rng.random((N, 8, 1, R))).astype(np.int64); at = 255 * (rng.random((N, 8, 16, L)) < rng.random((N, 8, 1, L))).astype(np.int64)
    at = np.where(rng.random((N, 8, 1, L)) < 0.3, 255 * rng.integers(0, 2, (N, 8, 1, L)), at)
    th = np.minimum(th + 700, 4080)
    key0[:, ::2] = rng.choice(np.array([0, 1, V - 2, V - 1]), (N, 4, L))
    ch[:, 4] = ch[:, 4, :1]
    for g in (3, 5):
        rec[:, g] = 255 * (rng.random((N, 1, R)) < 0.1); rec[:, g, :, R - 1458:R - 1455] = 0
        at[:, g] = 255 * (rng.random((N, 1, L)) < 0.9)
        ch[:, g] = rng.choice(np.array([0, R - 1, R - 1456, R - 1457, R - 1458]), (N, 16, V))
    th[:, 3] = 4079; th[:, 5] = rng.choice(np.array([0, 4079, 4080]), (N, 16, 1))
    w[:, 1] = 15
    rec[:, 1] = np.abs(255 * (rng.random((N, 16, R)) < 0.05) - rng.integers(0, 8, (N, 16, R)))
    at[:, 1] = np.abs(255 * (rng.random((N, 16, L)) < 0.6 + 0.4 * rng.random((N, 1, L))) - rng.integers(0, 8, (N, 16, L)))
    ch[:, 1, :, V - 1] = 0; rec[:, 1, :, 0] = 0; at[:, 1, :, 0] = 255; key0[:, 1, 0] = V - 1
    s = np.arange(N)[:, None] * L + np.argsort(rng.random((N, L)), axis=1) + 1
    turn = (np.arange(16)[None, :, None] + rng.integers(0, 16, (N, 1, L))) % 16
    at[:, 7] = s[:, None, :] // 16 + (turn < s[:, None, :] % 16); key0[:, 7] = s - 1
    rec[0, 7, :, :R - M] = 255; rec[0, 7, :, R - M:] = 0; ch[0, 7, 0] = R - M - 1
    th[0, 7] = 4080; th[0, 7, 0] = 2048; w[0, 7] = 0; w[0, 7, 0] = 1; th[1, 7] = 0
    return pack(rec, ch, at, key0, th, w)
def setup_inputs_quiet(rng):
    rec, ch, at, key0, th, w = parts(rng); q = rng.permutation(N)
    th[q[0]] = 4080; th[q[1]] = 0; th[:, rng.integers(0, 8)] = 4080; w[q[2]] = 15
    return pack(rec, ch, at, key0, th, w)
def setup_inputs_spread(rng):
    rec, ch, at, key0, th, w = parts(rng)
    rec = np.minimum((np.exp2(8 * rng.random((N, 8, 1, R))) * rng.random((N, 8, 16, R))).astype(np.int64), 255)
    at = np.minimum((np.exp2(8 * rng.random((N, 8, 1, L))) * rng.random((N, 8, 16, L))).astype(np.int64), 255)
    th = np.where(rng.random((N, 8, 16, 1)) < 0.1, rng.integers(0, 4081, (N, 8, 16, 1)), rng.integers(1200, 4081, (N, 8, 16, 1)))
    w = w * (rng.random((N, 8, 16, 1)) < 0.6)
    return pack(rec, ch, at, key0, th, w)
def setup_inputs_ties(rng):
    rec, ch, at, key0, th, w = parts(rng); u = rng.permutation(np.array([1, 1, 1, 2, 7, 16, 100, 255])).reshape(1, 8, 1, 1)
    rec = u * (rng.random((N, 8, 16, R)) < rng.random((N, 8, 1, R))); at = u * (rng.random((N, 8, 16, L)) < rng.random((N, 8, 1, L)))
    th = u * rng.integers(10, 15, (N, 8, 16, 1)) - rng.integers(0, 2, (N, 8, 16, 1))
    g = int(rng.integers(0, 8)); z = 255 * rng.integers(0, 2, 16); at[:, g] = z[:, None]
    th[:2, g] = 0; w[0, g] = 0
    e1, e2 = [R // 3 + int(i) for i in rng.integers(-150, 151, 2)]; steps = [e1, e2, R - e1 - e2]
    cs = [int(rng.integers(0, 100)), int(rng.integers(100, 200)), R - 1 - int(rng.integers(0, 100))]
    rec[1, g, :, 300] = z; ch[1, g, :, 0] = 300
    places = np.sort(rng.permutation(16)[:3])
    for i in range(3):
        far = int(np.nonzero(((37 * np.arange(M) + 1) & (M - 1)) == steps[i])[0][0])
        rec[1, g, :, cs[i]] = np.abs(z - (far // 16 + (np.arange(16) < far % 16)))
        rec[1, g, :, (cs[i] + steps[i]) % R] = z
        ch[1, g, places[i], 0] = cs[i]
    rec[0, g, 0, 1:] = 255 - z[0]; rec[0, g, :, 0] = z
    ch[0, g] = np.where(np.arange(V)[None, :] % 2 == 0, 0, rng.integers(1, R, (16, V)))
    key0[:, g] = 2 * rng.integers(0, V // 2, (N, L)); key0[2:N - 1, g] += 1; key0[1, g, 0] = 0
    return pack(rec, ch, at, key0, th, w)
def check_inputs(d):
    bad = []
    for k, hi in (("rec", 255), ("ch", R - 1), ("at", 255), ("key0", V - 1), ("th", 4080), ("w", 15)):
        v = np.asarray(d[k]).astype(np.float64)
        if not np.all((v >= 0) & (v <= hi) & (v == np.floor(v))): bad.append("range of " + k)
    return bad
def reference(rec, ch, at, key0, th, w):
    x = rec.astype(np.float32).astype(np.int32).reshape(N, 8, 16, R); a = at.astype(np.float32).astype(np.int32).reshape(N, 8, 16, L)
    c0 = ch.astype(np.int32).reshape(N, 8, 16, V); c = np.array(c0); lim = th.astype(np.int32).reshape(N, 8, 16, 1); wt = w.astype(np.int32).reshape(N, 8, 16, 1)
    k0 = np.stack([gentries(q) for q in key0]).astype(np.int64)
    key = np.array(k0); mark = np.zeros((N, 8, L), bool)
    low = np.tri(L, L, -1).astype(bool)
    for t in range(T):
        for b in range(N):
            r = (b + t) % N
            if t == 0 or r == 0:
                key[b] = k0[b]; mark[b] = False
            k = np.array(key[b]); m = np.array(mark[b])
            old = np.take_along_axis(c[r], k[:, None, :], 2)
            rows = np.take_along_axis(x[r], old.reshape(8, 1, 16 * L), 2).reshape(8, 16, 16, L)
            d = np.add.reduce(np.abs(rows - a[b][:, :, None, :]), axis=1)
            fail = d > lim[r]; bad = np.any(fail, axis=1); first = np.argmax(fail, axis=1)
            step = old + ((37 * d + 1) & (M - 1)); step = np.where(step >= R, step - R, step)
            mended = np.where(np.arange(16)[None, :, None] == first[:, None, :], step, old)
            back = np.take_along_axis(c0[r], k[:, None, :], 2)
            col = np.where(m[:, None, :], back, mended)
            want = m | bad
            lost = np.any((k[:, :, None] == k[:, None, :]) & want[:, None, :] & low[None], axis=2)
            win = want & ~lost
            for g in range(8):
                jj = np.nonzero(win[g])[0]
                c[r, g][:, k[g, jj]] = col[g][:, jj]
            mark[b] = m | win
            key[b] = np.add.reduce(wt[r] * d, axis=1) & (V - 1)
    end = [(r - (T - 1)) % N for r in range(N)]
    return {"yc": c.reshape(N, 128, V).astype(np.float32), "yk": np.stack([key[b] + V * mark[b] for b in end]).astype(np.float32)}

@@ -1,0 +1,425 @@
+from concourse.mybir import AluOpType as A, ActivationFunctionType as F
+
+V, R, L, ROUNDS, N = 2048, 4096, 256, 8, 4
+CHUNKS = (64, 64, 64, 64)
+MODES = "RPPQ"
+ORDER = ("n1 g0 M g1 base n0 b0 s0 b1 g2 f0 um s1 g3 p0 b2 n2 b3 f1 r3 r1 r2 r4 s2 p1 f2 h02 n3 r7 r5 p2 r12 s3 m02 "
+         "r9 r6 f3 r8 p3 r10 h33 r13 r15 K m33 r14 r11 W")
+
+SCRATCH = {n: ("sbuf", s, d) for d, s, names in (
+    ("bfloat16", [128, R], "recs ax0 ax1 ax2 ax3 diff absd"),
+    ("bfloat16", [128, L], "atom sgn zero"),
+    ("bfloat16", [128, 16, 17], "first mrow"),
+    ("bfloat16", [128, 16, L], "junk"),
+    ("bfloat16", [128, 128], "ones c1 c2 c3 blk eye eyem eyeu low blku blkd xm"),
+    ("bfloat16", [128, 144], "slide sliden slidew"),
+    ("bfloat16", [128, 16, 128], "sel seld"),
+    ("bfloat16", [128, 272], "ownr m1"),
+    ("float16", [128, 128], "eyed maskt"),
+    ("float16", [128, ROUNDS * 32], "lh"),
+    ("float16", [128, L], "dh"),
+    ("float16", [128, 16], "vh"),
+    ("uint16", [128, ROUNDS * 32], "lu"),
+    ("uint16", [128, L], "cand"),
+    ("uint16", [128, 16], "ou"),
+    ("int32", [128, V], "chi"),
+    ("int32", [128, L], "xi ei si col"),
+    ("int32", [128, 16], "k0i ti zi k1 k2"),
+    ("int32", [128, 4], "thi wi pi pj"),
+    ("float32", [128, 2 * V + L], "tab"),
+    ("float32", [128, ROUNDS, 32], "inbox outbox"),
+    ("float32", [128, L], "basef vrow"),
+    ("float32", [128, 272], "seed prod"),
+    ("float32", [128, 128], "c4 c5 eyef"),
+    ("float32", [128, 16], "tsum tb kq nw o0 o1 o2 ums um lost nm i16 lane laneq own lo hi"),
+    ("float32", [128, 8], "cols"),
+) for n in names.split()}
+SCRATCH.update({"pd": ("psum", [128, 4, 512], "float32")})
+SCRATCH.update({n: ("psum", [128, 512], "float32") for n in ("pz", "pu", "pq", "pk")})
+SEMAPHORES = (["v", "a", "p", "gp", "l_at", "l_k0", "l_th", "l_w", "l_ch", "l_rec", "sent", "st_c", "st_k"]
+              + ["key%d" % t for t in range(1, ROUNDS)] + ["mark%d" % t for t in range(1, ROUNDS)]
+              + ["tile%d" % k for k in range(1, N)])
+BANKS = ("pd0", "pd1", "pd2", "pd3", "pz", "pu", "pq", "pk")
+
+
+def rank_program(g, core, T, topo):
+    r = T.rank_of(core)
+    if r is None:
+        return
+    queue = {"v": g.vector, "a": g.scalar, "p": g.tensor, "gp": g, "s": g.sync}
+    count = {"v": 0, "a": 0, "p": 0, "gp": 0}
+    known = {e: {} for e in queue}
+    clock = {}
+    writer, readers, bank = {}, {}, {b: {} for b in BANKS}
+
+    def wait(e, deps):
+        need = {}
+        for s, n in deps:
+            need[s] = max(need.get(s, 0), n)
+        todo = [(s, n) for s, n in need.items() if known[e].get(s, 0) < n]
+        for s, n in todo:
+            if any(clock.get(o, {}).get(s, 0) >= n for o in todo if o != (s, n)):
+                continue
+            queue[e].wait_ge(T.sem[s], n)
+        for s, n in todo:
+            known[e][s] = max(known[e].get(s, 0), n)
+            for s2, n2 in clock.get((s, n), {}).items():
+                known[e][s2] = max(known[e].get(s2, 0), n2)
+
+    def deps_of(e, rd, wr):
+        deps = []
+        for x in rd:
+            if x in writer:
+                deps.append(writer[x])
+        for x in wr:
+            if x in writer:
+                deps.append(writer[x])
+            deps += readers.get(x, [])
+        for x in list(rd) + list(wr):
+            b = x.split(":")[0]
+            if b in bank:
+                deps += [(o, n) for o, n in bank[b].items() if o != e]
+        if e == "p":
+            deps = [d for d in deps if d[0] != "p"]
+        return deps
+
+    def note(tag, rd, wr):
+        for x in rd:
+            readers.setdefault(x, []).append(tag)
+        for x in wr:
+            writer[x] = tag
+            readers[x] = []
+
+    def op(e, call, rd, wr):
+        wait(e, deps_of(e, rd, wr))
+        call().then_inc(T.sem[e], 1)
+        count[e] += 1
+        tag = (e, count[e])
+        clock[tag] = dict(known[e])
+        note(tag, rd, wr)
+        for x in list(rd) + list(wr):
+            b = x.split(":")[0]
+            if b in bank:
+                bank[b][e] = count[e]
+
+    def dma(e, sem, out, in_, rd, wr):
+        wait(e, deps_of(e, rd, wr))
+        queue[e].dma_start(out, in_).then_inc(T.sem[sem], 16)
+        clock[(sem, 16)] = dict(known[e])
+        note((sem, 16), rd, wr)
+
+    sent = [0]
+
+    def send(to, out, in_, sem, small, rd):
+        dst = T.cores[to]
+        eng = topo.engines(core, dst)
+        half = len(eng) // 2
+        use = eng[:half] if small else eng[half:]
+        rid, pid = topo.addr(dst)[:2]
+        wait("gp", deps_of("gp", rd, []))
+        g.remote_dma(out, in_, T.sem[sem], T.sem.sent, pid, rid, sum(1 << x for x in use))
+        sent[0] += len(use)
+
+    def arrives(name, sem, frm):
+        writer[name] = (sem, len(topo.engines(T.cores[frm], core)) // 2)
+
+    v, a, p = g.vector, g.scalar, g.tensor
+
+    def ts(out, in0, s1, op0, rd, wr, s2=None, op1=None):
+        if op1 is None:
+            op("v", lambda: v.tensor_scalar(out, in0, s1, None, op0), rd, wr)
+        else:
+            op("v", lambda: v.tensor_scalar(out, in0, s1, s2, op0, op1), rd, wr)
+
+    def tt(out, in0, in1, o, rd, wr):
+        op("v", lambda: v.tensor_tensor(out, in0, in1, o), rd, wr)
+
+    def cp(out, in_, rd, wr):
+        op("v", lambda: v.tensor_copy(out, in_), rd, wr)
+
+    def fill(ap, c, wr):
+        op("v", lambda: v.memset(ap, c), [], wr)
+
+    def act(out, in_, f, rd, wr, **kw):
+        op("a", lambda: a.activation(out, in_, f, **kw), rd, wr)
+
+    def mm(out, lhs, rhs, start, stop, rd, wr):
+        op("p", lambda: p.matmul(out, lhs, rhs, start, stop), rd, wr)
+
+    def gp(call, rd, wr):
+        op("gp", call, rd, wr)
+
+    dma("s", "l_at", T.atom[:], T.at[:], [], ["atom"])
+    dma("a", "l_k0", T.k0i[:], T.key0[:], [], ["k0i"])
+    dma("s", "l_ch", T.chi[:], T.ch[:], [], ["chi"])
+    dma("a", "l_th", T.thi[:, 0:1], T.th[:], [], ["thi"])
+    dma("a", "l_w", T.wi[:, 0:1], T.w[:], [], ["wi"])
+    dma("s", "l_rec", T.recs[:], T.rec[:], [], ["recs"])
+    for k in range(1, N):
+        arrives("ax%d" % k, "tile%d" % k, (r - k) % N)
+    for t in range(1, ROUNDS):
+        if r > 0:
+            arrives("key%d" % t, "key%d" % t, r - 1)
+            arrives("km%d" % t, "mark%d" % t, r - 1)
+        elif t < N:
+            arrives("key%d" % t, "key%d" % t, N - t)
+            arrives("km%d" % t, "key%d" % t, N - t)
+
+    fill(T.ones[:], 1.0, ["ones"])
+    gp(lambda: g.iota(T.pi[:, 0:1], [[0, 1]], 0, 1), [], ["pi"])
+    gp(lambda: g.iota(T.i16[:], [[1, 16]], 0, 0, allow_small_or_imprecise_dtypes=True), [], ["i16"])
+    gp(lambda: g.affine_select(T.eye[:], T.ones[:], [[-1, 128]], A.is_equal, 0.0, 0, 1), ["ones"], ["eye"])
+    gp(lambda: g.affine_select(T.c1[:], T.ones[:], [[-16, 8], [0, 16]], A.is_ge, 0.0, 0, 1), ["ones"], ["c1"])
+    gp(lambda: g.affine_select(T.blk[:], T.c1[:], [[16, 8], [0, 16]], A.is_ge, 0.0, 15, -1), ["c1"], ["blk"])
+    gp(lambda: g.affine_select(T.c3[:], T.blk[:], [[1, 128]], A.is_gt, 0.0, 0, -1), ["blk"], ["c3"])
+    gp(lambda: g.iota(T.m1[:], [[0, 16], [1, 17]], -1, 0, allow_small_or_imprecise_dtypes=True), [], ["m1"])
+    fill(T.seed[:], 0.0, ["seed"])
+    act(T.seed[:, 0::17], T.ones[:, 0:16], F.Tanh, ["ones", "seed"], ["seed"], scale=16.0)
+    fill(T.slide[:], 0.0, ["slide"])
+    fill(T.zero[:], 0.0, ["zero"])
+    ts(T.pj[:, 0:1], T.pi[:, 0:1], 15, A.bitwise_and, ["pi"], ["pj"])
+    fill(T.tsum[:], 0.0, ["ts%d" % j for j in range(16)])
+    cp(T.cols[:, 0:1], T.pj[:, 0:1], ["pj"], ["c_pl"])
+    ts(T.cols[:, 1:2], T.pj[:, 0:1], -37.0, A.mult, ["pj"], ["c_fb"], -37 * 18.5, A.add)
+    ts(T.own[:], T.i16[:], T.cols[:, 0:1], A.is_equal, ["i16", "c_pl"], ["own"])
+    ts(T.lane[:], T.i16[:], 16.0, A.mult, ["i16", "c_pl"], ["lane"], T.cols[:, 0:1], A.add)
+    fill(T.first[:, :, 0], 0.0, ["first_0"])
+    ts(T.hi[:], T.own[:], 1.0 / 64, A.mult, ["own"], ["hi"])
+    ts(T.lo[:], T.own[:], -1.0, A.add, ["own"], ["lo"], 1.0 / 64, A.mult)
+    fill(T.mrow[:, :, 0], 0.0, ["mrow_0"])
+    ts(T.laneq[:], T.lane[:], 1.0 / R, A.mult, ["lane"], ["laneq"])
+    fill(T.tab[:, 2 * V:], 0.0, ["spare"])
+    ts(T.inbox[:, 0, 0:16], T.k0i[:], -2048.0, A.add, ["k0i"], ["key0"])
+    cp(T.inbox[:, 0, 16:32], T.k0i[:], ["k0i"], ["km0"])
+    if r > 0:
+        send(0, T.inbox[:, N - r, :], T.inbox[:, 0, :], "key%d" % (N - r), True, ["key0", "km0"])
+    act(T.c2[:], T.eye[:], F.Identity, ["eye"], ["c2"], scale=-2.0)
+    act(T.eyem[:], T.eye[:], F.Identity, ["eye"], ["eyem"], scale=18.5)
+    act(T.eyeu[:], T.eye[:], F.Identity, ["eye"], ["eyeu"], scale=160.0)
+    act(T.eyef[:], T.eye[:], F.Copy, ["eye"], ["eyef"])
+    act(T.blku[:], T.blk[:], F.Identity, ["blk"], ["blku"], scale=-64.0)
+    act(T.blkd[:], T.blk[:], F.Identity, ["blk"], ["blkd"], scale=-1.0)
+    tt(T.c1[:], T.blk[:], T.c2[:], A.add, ["blk", "c2"], ["c1"])
+    tt(T.low[:], T.eye[:], T.c3[:], A.subtract, ["eye", "c3"], ["low"])
+    ts(T.xm[:], T.c1[:], 1.0 / 64, A.mult, ["c1"], ["xm"])
+    for i in range(16):
+        if i < 10:
+            cp(T.ax0[:, i::16], T.atom[:], ["atom"], ["ax0_%d" % i])
+        else:
+            act(T.ax0[:, i::16], T.atom[:], F.Copy, ["atom"], ["ax0_%d" % i])
+    ax0 = ["ax0_%d" % i for i in range(16)]
+    ts(T.slide[:, 15:143:16], T.blk[:, 0::16], 2.0, A.mult, ["blk", "slide"], ["slide"])
+    if MODES.count("P") < len(MODES):
+        act(T.sliden[:], T.slide[:], F.Identity, ["slide"], ["sliden"], scale=-0.5)
+    ts(T.cols[:, 2:3], T.thi[:, 0:1], -1.0, A.mult, ["thi"], ["c_th"], -941.5, A.add)
+    cp(T.cols[:, 3:4], T.wi[:, 0:1], ["wi"], ["c_w"])
+    ts(T.eyed[:], T.eye[:], 941.0, A.mult, ["eye"], ["eyed"])
+    ts(T.ownr[:], T.m1[:], T.cols[:, 0:1], A.is_equal, ["m1", "c_pl"], ["ownr"])
+    ts(T.slidew[:], T.slide[:], T.cols[:, 3:4], A.mult, ["slide", "c_w"], ["slidew"], 0.5, A.mult)
+    act(T.c4[:], T.c1[:], F.Identity, ["c1"], ["c4"], scale=5 * 18.5)
+    act(T.c5[:], T.low[:], F.Identity, ["low"], ["c5"], scale=4 * 18.5)
+    for il in range(16):
+        act(T.sel[:, il, :], T.blk[:], F.Identity, ["blk", "own"], ["sel%d" % il], scale=T.own[:, il:il + 1])
+        ts(T.seld[:, il, :], T.xm[:], T.lo[:, il:il + 1], A.max, ["xm", "lo", "hi"], ["seld%d" % il],
+           T.hi[:, il:il + 1], A.min)
+    tt(T.maskt[:], T.c4[:], T.c5[:], A.add, ["c4", "c5"], ["maskt"])
+    cp(T.tab[:, V:2 * V], T.chi[:], ["chi"], ["tab"])
+    act(T.tab[:, 0:V], T.tab[:, V:2 * V], F.Copy, ["tab"], ["ch0"])
+    wait("gp", [writer["recs"]])
+    for k in range(1, N):
+        send((r + k) % N, T["ax%d" % k][:], T.ax0[:], "tile%d" % k, False, ax0)
+
+    table = T.tab[:, V:2 * V + L]
+    edges = [0]
+    for n in CHUNKS:
+        edges.append(edges[-1] + n)
+
+    def lists(t):
+        slot = t if r > 0 else t % N
+        both = t == 0 or r == 0
+        w0, c0 = (32 if both else 16), 32 * t
+        src = ["key%d" % slot] + (["km%d" % slot] if both else [])
+        ts(T.lu[:, c0:c0 + w0], T.inbox[:, slot, 0:w0], 2048.0, A.add, src, ["luk%d" % t] + (["lum%d" % t] if both else []))
+        cp(T.lh[:, c0:c0 + w0], T.inbox[:, slot, 0:w0], src, ["lhk%d" % t] + (["lhm%d" % t] if both else []))
+
+    def rows(lst, name):
+        mm(T.pu[:, L:2 * L], T.eye[:], T.zero[:], True, False, ["eye", "zero"], ["pu:r"])
+        for il in range(16):
+            mm(T.pu[:, L + il:2 * L:16], T.sel[:, il, :], lst, False, il == 15, ["sel%d" % il, name], ["pu:r"])
+
+    def weave(*chains):
+        chains = list(chains)
+        while chains:
+            chains = [c for c in chains if next(c, 0) is None]
+
+    for t in range(ROUNDS):
+        last = t == ROUNDS - 1
+        out_keys = last or r < N - 1
+        slot = t if r > 0 else t % N
+        kn, mn = "key%d" % slot, "km%d" % slot
+        luk, lum, lhk, lhm = ["%s%d" % (x, t) for x in ("luk", "lum", "lhk", "lhm")]
+        keyp, km = T.inbox[:, slot, 0:16], T.inbox[:, slot, 16:32]
+        c0 = 32 * t
+        ax, axn = T["ax%d" % (t % N)], (ax0 if t % N == 0 else ["ax%d" % (t % N)])
+        both = t == 0 or r == 0
+        on = "out%d" % t
+
+        lists(t)
+        cp(T.cand[:], table.indirect(T.lu[:, c0:c0 + 16]), ["tab", "spare", luk], ["cand"])
+        act(T.tb[:], keyp, F.Identity, [kn], ["tb"], scale=-8.0, bias=1280 + 1.0 / 512)
+        act(T.kq[:], keyp, F.Identity, [kn], ["kq"], scale=1.0 / R)
+        mm(T.pq[:, 0:272], T.maskt[:], T.ownr[:], True, False, ["maskt", "ownr"], ["pq"])
+        for il in range(16):
+            mm(T.pq[:, 1 + il:272:17], T.seld[:, il, :], T.lh[:, c0:c0 + 16], False, False, ["seld%d" % il, lhk], ["pq"])
+
+        def marks():
+            if not both:
+                cp(T.lh[:, c0 + 16:c0 + 32], km, [mn], [lhm])
+                ts(T.lu[:, c0 + 16:c0 + 32], km, 2048.0, A.add, [mn], [lum])
+            rows(T.lh[:, c0 + 16:c0 + 32], lhm)
+            act(T.mrow[:, :, 1:17], T.pu[:, L:2 * L], F.Sign, ["pu:r"], ["mrow"], bias=0.5)
+            act(T.vrow[:], T.pu[:, L:2 * L], F.Copy, ["pu:r"], ["vrow"])
+            mm(T.pq[:, 0:272], T.eyem[:], T.mrow[:], False, False, ["eyem", "mrow", "mrow_0"], ["pq"])
+
+        def base():
+            act(T.basef[:], T.tab[:, 0:2 * V].indirect(T.lu[:, c0 + 16:c0 + 32]), F.Copy, ["tab", "ch0", lum], ["base"])
+
+        def gather(c):
+            l0, l1 = edges[c], edges[c + 1]
+            out, x = T.diff[:, 16 * l0:16 * l1], T.recs[:].indirect(T.cand[:, l0:l1])
+            if MODES[c] == "R":
+                act(out, x, F.Copy, ["recs", "cand"], ["diff%d" % c])
+            else:
+                tt(out, x, ax[:, 16 * l0:16 * l1], A.subtract, ["recs", "cand"] + axn, ["diff%d" % c])
+
+        def absval(c):
+            l0, l1 = edges[c], edges[c + 1]
+            out, x = T.absd[:, 16 * l0:16 * l1], T.diff[:, 16 * l0:16 * l1]
+            if MODES[c] == "R":
+                tt(out, x, ax[:, 16 * l0:16 * l1], A.max, ["diff%d" % c] + axn, ["abs%d" % c])
+            elif MODES[c] == "Q":
+                ts(out, x, 0.0, A.max, ["diff%d" % c], ["abs%d" % c])
+            else:
+                act(out, x, F.Abs, ["diff%d" % c], ["abs%d" % c], scale=0.5)
+
+        def negs(s):
+            mm(T.pd[:, s, 0:64], T.eyed[:], T.ones[:, 0:64], True, False, ["eyed", "ones"], ["pd%d" % s])
+            cs = [c for c in range(len(CHUNKS)) if edges[c] // 64 == s and MODES[c] != "P"]
+            if cs:
+                l0, l1 = edges[cs[0]], edges[cs[-1] + 1]
+                o = T.pd[:, s, l0 - 64 * s:l1 - 64 * s]
+                if MODES[cs[0]] == "R":
+                    mm(o, T.blkd[:], ax[:, 16 * l0:16 * l1:16], False, False, ["blkd"] + axn, ["pd%d" % s])
+                for i in range(16):
+                    mm(o, T.sliden[:, 15 - i:143 - i], T.diff[:, 16 * l0 + i:16 * l1:16], False, False,
+                       ["sliden"] + ["diff%d" % c for c in cs], ["pd%d" % s])
+
+        def sums(s):
+            l0, l1 = 64 * s, 64 * s + 64
+            src = ["abs%d" % c for c in range(len(CHUNKS)) if edges[c] < l1 and edges[c + 1] > l0]
+            for i in range(16):
+                mm(T.pd[:, s, 0:64], T.slide[:, 15 - i:143 - i], T.absd[:, 16 * l0 + i:16 * l1:16], False, i == 15,
+                   ["slide"] + src, ["pd%d" % s])
+
+        def fails(s):
+            l0, l1 = 64 * s, 64 * s + 64
+            act(T.sgn[:, l0:l1], T.pd[:, s, 0:64], F.Sign, ["pd%d" % s, "c_th"], ["sgn%d" % s], bias=T.cols[:, 2:3])
+            mm(T.pz[:, l0:l1], T.eyem[:], T.mrow[:, 4 * s:4 * s + 4, 1:17], True, False, ["eyem", "mrow"], ["pz:%d" % s])
+            mm(T.pz[:, l0:l1], T.low[:], T.sgn[:, l0:l1], False, True, ["low", "sgn%d" % s], ["pz:%d" % s])
+
+        def first(s):
+            l0, l1 = 64 * s, 64 * s + 64
+            fs = T.first[:, 4 * s:4 * s + 4, 1:17]
+            act(fs, T.pz[:, l0:l1], F.Relu, ["pz:%d" % s, "c_fb"], ["first%d" % s], scale=37.0, bias=T.cols[:, 1:2])
+            mm(T.pu[:, l0:l1], T.eyef[:], T.vrow[:, l0:l1], True, False, ["eyef", "vrow"], ["pu:%d" % s])
+            mm(T.pu[:, l0:l1], T.eyeu[:], T.mrow[:, 4 * s:4 * s + 4, 1:17], False, False, ["eyeu", "mrow"], ["pu:%d" % s])
+            mm(T.pq[:, 68 * s:68 * s + 68], T.blkd[:], T.first[:, 4 * s:4 * s + 4, :], False, s == 3,
+               ["blkd", "first%d" % s, "first_0"], ["pq"])
+            mm(T.pu[:, l0:l1], T.blku[:], fs, False, True, ["blku", "first%d" % s], ["pu:%d" % s])
+
+        def rivals(j):
+            src = ["pu:%d" % s for s in range(4) if 64 * s < 16 * j]
+            act(T.junk[:, j, 0:16 * j], T.pu[:, 0:16 * j], F.Tanh, src + ["tb"], ["junk%d" % j, "ts%d" % j],
+                scale=8.0, bias=T.tb[:, j:j + 1], accum_out=T.tsum[:, j:j + 1])
+
+        def mend(s0, s1):
+            l0, l1 = 64 * s0, 64 * s1 + 64
+            ss = range(s0, s1 + 1)
+            yield tt(T.xi[:, l0:l1], T.pd[:, s0:s1 + 1, 0:64], T.first[:, 4 * s0:4 * s1 + 4, 1:17], A.mult,
+                     ["pd%d" % s for s in ss] + ["first%d" % s for s in ss], ["xi%d" % s0])
+            yield ts(T.ei[:, l0:l1], T.xi[:, l0:l1], 2047, A.bitwise_and, ["xi%d" % s0], ["ei%d" % s0])
+            yield tt(T.si[:, l0:l1], T.ei[:, l0:l1], T.basef[:, l0:l1], A.add, ["ei%d" % s0, "base"], ["si%d" % s0])
+            yield ts(T.col[:, l0:l1], T.si[:, l0:l1], R - 1, A.bitwise_and, ["si%d" % s0], ["col%d" % s for s in ss])
+
+        def half(s0, s1):
+            if out_keys:
+                ts(T.dh[:, 64 * s0:64 * s1 + 64], T.pd[:, s0:s1 + 1, 0:64], -2989.0, A.add,
+                   ["pd%d" % s for s in range(s0, s1 + 1)], ["dh%d" % s for s in range(s0, s1 + 1)])
+
+        def key_sums():
+            if out_keys:
+                for jl in range(16):
+                    mm(T.pk[:, 0:16], T.slidew[:, 15 - jl:143 - jl], T.dh[:, jl::16], jl == 0, jl == 15,
+                       ["slidew", "dh0", "dh1", "dh2", "dh3"], ["pk"])
+
+        def keys():
+            if out_keys:
+                yield ts(T.k1[:], T.pk[:, 0:16], 524288.0, A.add, ["pk"], ["k1"])
+                yield ts(T.k2[:], T.k1[:], V - 1, A.bitwise_and, ["k1"], ["k2"])
+                yield ts(T.outbox[:, t, 0:16], T.k2[:], -2048.0, A.add, ["k2"], [on + "k"])
+                if not last:
+                    send(r + 1, T.inbox[:, t + 1, 0:16], T.outbox[:, t, 0:16], "key%d" % (t + 1), True, [on + "k"])
+
+        def block():
+            yield op("v", lambda: v.tensor_tensor_scan(T.prod[:], T.pq[:, 0:272], T.seed[:], 0.0, A.mult, A.add),
+                     ["pq", "seed"], ["prod"])
+            yield ts(T.nw[:], T.prod[:, 16::17], 0.0, A.is_equal, ["prod"], ["nw"])
+            yield tt(T.o0[:], T.nw[:], T.kq[:], A.add, ["nw", "kq"], ["o0"])
+
+        def write():
+            ts(T.ti[:], T.tsum[:], 512.0, A.mult, ["ts%d" % j for j in range(16)], ["ti"])
+            ts(T.zi[:], T.ti[:], 511, A.bitwise_and, ["ti"], ["zi"])
+            tt(T.o1[:], T.o0[:], T.zi[:], A.add, ["o0", "zi"], ["o1"])
+            tt(T.o2[:], T.o1[:], T.laneq[:], A.min, ["o1", "laneq"], ["o2"])
+            if out_keys:
+                ts(T.lost[:], T.o2[:], 0.0, A.is_ge, ["o2"], ["lost"], 2048.0, A.mult)
+            ts(T.ou[:], T.o2[:], float(R), A.mult, ["o2"], ["ou"], 2048.0, A.add)
+            if out_keys:
+                tt(T.nm[:], T.lost[:], T.um[:], A.min, ["lost", "um"], ["nm"])
+                if not last:
+                    tt(T.outbox[:, t, 16:32], T.nm[:], T.outbox[:, t, 0:16], A.add, ["nm", on + "k"], [on + "m"])
+                    send(r + 1, T.inbox[:, t + 1, 16:32], T.outbox[:, t, 16:32], "mark%d" % (t + 1), True, [on + "m"])
+            cp(table.indirect(T.ou[:]), T.col[:], ["ou"] + ["col%d" % s for s in range(4)], ["tab", "spare"])
+
+        for w in ORDER.split():
+            k, n = w[0], w[1:]
+            if w == "M":
+                marks()
+            elif w == "base":
+                base()
+            elif w == "um":
+                if out_keys:
+                    act(T.ums[:], km, F.Sign, [mn], ["ums"], bias=0.5)
+                    act(T.um[:], T.ums[:], F.Identity, ["ums"], ["um"], scale=1024.0, bias=1024.0)
+            elif w == "K":
+                key_sums()
+            elif w == "W":
+                write()
+            elif k == "m":
+                if n[1] == "3":
+                    weave(mend(int(n[0]), 3), block(), keys())
+                else:
+                    weave(mend(int(n[0]), int(n[1])))
+            elif k == "h":
+                half(int(n[0]), int(n[1]))
+            else:
+                {"g": gather, "b": absval, "n": negs, "s": sums, "f": fails, "p": first, "r": rivals}[k](int(n))
+
+    dma("s", "st_c", T.yc[:], T.tab[:, V:2 * V], ["tab"], [])
+    tt(T.o1[:], T.outbox[:, ROUNDS - 1, 0:16], T.nm[:], A.subtract, ["out%dk" % (ROUNDS - 1), "nm"], ["o1"])
+    ts(T.vh[:], T.o1[:], 2048.0, A.add, ["o1"], ["vh"])
+    rows(T.vh[:], "vh")
+    act(T.vrow[:], T.pu[:, L:2 * L], F.Identity, ["pu:r"], ["vrow"], bias=2048.0)
+    dma("a", "st_k", T.yk[:], T.vrow[0:128:16, :], ["vrow"], [])
+    g.wait_ge(T.sem.sent, sent[0])
+    wait("gp", [(e, n) for e, n in count.items()] + [("st_c", 16), ("st_k", 16)])

@@ -1,45 +1,55 @@
 from concourse.mybir import AluOpType as A, ActivationFunctionType as F
 
 V, R, L, ROUNDS, N = 2048, 4096, 256, 8, 4
-CHUNKS = (64, 64, 64, 64)
-MODES = "RPPQ"
-ORDER = ("n1 g0 M g1 base n0 b0 s0 b1 g2 f0 um s1 g3 p0 b2 n2 b3 f1 r3 r1 r2 r4 s2 p1 f2 h02 n3 r7 r5 p2 r12 s3 m02 "
-         "r9 r6 f3 r8 p3 r10 h33 r13 r15 K m33 r14 r11 W")
+CUT = 192
+PIECES = ((0, 64, "R"), (64, 128, "P"), (128, 192, "R"), (192, 224, "Q"), (224, 256, "Q"))
+SUMS = ((0, 64), (64, 128), (128, 192), (192, 256))
+CANDS = ((0, 64), (64, 256))
+STAGES = {"a": (0, 128), "b": (128, 192), "c": (192, 256)}
+MENDS = {"A": (0, 192), "B": (192, 256)}
+DH_SCALAR = ""
+ORDER = ("c0 kx c1 g0 qA g2 g1 kmu b0 qB M b2 l0 s0 l1 l2 b1 s2 M g3 sg.b g4 s1 M u.a sg.a sg.b dh.a sg.a fi.a b4 fi.a "
+         "fi.b u.b tb fi.b r13 b3 l3 r5 xi.b xi.a mA s3 r14 qA dh.b r12 r4 sg.c sg.c u.c r7 mA fi.c r2 dh.c fi.c xi.c "
+         "e13 r15 zB fi.a qB fi.b r8 K fi.c e15 r10 mA e14 mB oA r11 zB r6 r3 r1 r9 oB K mB zA zB K mB um zA oB zA K "
+         "oB oA WB oA nm WA nm ku nm")
+HALVES = 1.5 * 2 ** 22
+WIDE = 1 + L - CUT
 
 SCRATCH = {n: ("sbuf", s, d) for d, s, names in (
     ("bfloat16", [128, R], "recs ax0 ax1 ax2 ax3 diff absd"),
-    ("bfloat16", [128, L], "atom sgn zero"),
+    ("bfloat16", [128, L], "atom sgn zero ones"),
     ("bfloat16", [128, 16, 17], "first mrow"),
     ("bfloat16", [128, 16, L], "junk"),
-    ("bfloat16", [128, 128], "ones c1 c2 c3 blk eye eyem eyeu low blku blkd xm"),
+    ("bfloat16", [128, 128], "c1 c2 c3 blk eye eyem eyeu low blku blkd xm"),
     ("bfloat16", [128, 144], "slide sliden slidew"),
     ("bfloat16", [128, 16, 128], "sel seld"),
     ("bfloat16", [128, 272], "ownr m1"),
-    ("float16", [128, 128], "eyed maskt"),
-    ("float16", [128, ROUNDS * 32], "lh"),
-    ("float16", [128, L], "dh"),
+    ("bfloat16", [128, CUT // 16 * 17], "hitA"),
+    ("bfloat16", [128, (L - CUT) // 16, WIDE], "hitB"),
+    ("float16", [128, 128], "eyed eyeh maskt"),
+    ("float16", [128, ROUNDS, 32], "inbox outbox"),
+    ("float16", [128, L], "dh vrow"),
     ("float16", [128, 16], "vh"),
     ("uint16", [128, ROUNDS * 32], "lu"),
     ("uint16", [128, L], "cand"),
     ("uint16", [128, 16], "ou"),
     ("int32", [128, V], "chi"),
     ("int32", [128, L], "xi ei si col"),
-    ("int32", [128, 16], "k0i ti zi k1 k2"),
+    ("int32", [128, 16], "k0i ti zi"),
     ("int32", [128, 4], "thi wi pi pj"),
-    ("float32", [128, 2 * V + L], "tab"),
-    ("float32", [128, ROUNDS, 32], "inbox outbox"),
-    ("float32", [128, L], "basef vrow"),
-    ("float32", [128, 272], "seed prod"),
-    ("float32", [128, 128], "c4 c5 eyef"),
-    ("float32", [128, 16], "tsum tb kq nw o0 o1 o2 ums um lost nm i16 lane laneq own lo hi"),
+    ("float32", [128, 2 * V + L + 8], "tab"),
+    ("float32", [128, L], "krow"),
+    ("float32", [128, CUT // 16 * 17], "capA endA"),
+    ("float32", [128, (L - CUT) // 16, WIDE], "capB endB"),
+    ("float32", [128, 128], "c4 c5"),
+    ("float32", [128, 16], "tsum tb kx um lost nm i16 own lo hi k1 k2"),
     ("float32", [128, 8], "cols"),
 ) for n in names.split()}
-SCRATCH.update({"pd": ("psum", [128, 4, 512], "float32")})
-SCRATCH.update({n: ("psum", [128, 512], "float32") for n in ("pz", "pu", "pq", "pk")})
-SEMAPHORES = (["v", "a", "p", "gp", "l_at", "l_k0", "l_th", "l_w", "l_ch", "l_rec", "sent", "st_c", "st_k"]
-              + ["key%d" % t for t in range(1, ROUNDS)] + ["mark%d" % t for t in range(1, ROUNDS)]
+BANKS = ("pda", "pdb", "pdc", "pz", "pu", "pr", "pqA", "pqB")
+SCRATCH.update({n: ("psum", [128, 512], "float32") for n in BANKS})
+SEMAPHORES = (["v", "a", "p", "gp", "l_at", "l_k0", "l_th", "l_w", "l_ch", "l_rec", "l_c0", "sent", "st_c", "st_k"]
+              + ["%s%d" % (x, t) for x in ("key", "mark") for t in range(1, ROUNDS)]
               + ["tile%d" % k for k in range(1, N)])
-BANKS = ("pd0", "pd1", "pd2", "pd3", "pz", "pu", "pq", "pk")
 
 
 def rank_program(g, core, T, topo):
@@ -67,10 +77,7 @@ def rank_program(g, core, T, topo):
                 known[e][s2] = max(known[e].get(s2, 0), n2)
 
     def deps_of(e, rd, wr):
-        deps = []
-        for x in rd:
-            if x in writer:
-                deps.append(writer[x])
+        deps = [writer[x] for x in rd if x in writer]
         for x in wr:
             if x in writer:
                 deps.append(writer[x])
@@ -110,14 +117,14 @@ def rank_program(g, core, T, topo):
 
     sent = [0]
 
-    def send(to, out, in_, sem, small, rd):
+    def send(to, out, in_, sems, small, rd):
         dst = T.cores[to]
         eng = topo.engines(core, dst)
         half = len(eng) // 2
         use = eng[:half] if small else eng[half:]
         rid, pid = topo.addr(dst)[:2]
         wait("gp", deps_of("gp", rd, []))
-        g.remote_dma(out, in_, T.sem[sem], T.sem.sent, pid, rid, sum(1 << x for x in use))
+        g.remote_dma(out, in_, T.sem[sems], T.sem.sent, pid, rid, sum(1 << x for x in use))
         sent[0] += len(use)
 
     def arrives(name, sem, frm):
@@ -151,57 +158,58 @@ def rank_program(g, core, T, topo):
 
     dma("s", "l_at", T.atom[:], T.at[:], [], ["atom"])
     dma("a", "l_k0", T.k0i[:], T.key0[:], [], ["k0i"])
-    dma("s", "l_ch", T.chi[:], T.ch[:], [], ["chi"])
-    dma("a", "l_th", T.thi[:, 0:1], T.th[:], [], ["thi"])
+    dma("s", "l_th", T.thi[:, 0:1], T.th[:], [], ["thi"])
     dma("a", "l_w", T.wi[:, 0:1], T.w[:], [], ["wi"])
+    dma("s", "l_ch", T.chi[:], T.ch[:], [], ["chi"])
     dma("s", "l_rec", T.recs[:], T.rec[:], [], ["recs"])
     for k in range(1, N):
         arrives("ax%d" % k, "tile%d" % k, (r - k) % N)
     for t in range(1, ROUNDS):
         if r > 0:
             arrives("key%d" % t, "key%d" % t, r - 1)
-            arrives("km%d" % t, "mark%d" % t, r - 1)
+            arrives("mark%d" % t, "mark%d" % t, r - 1)
         elif t < N:
             arrives("key%d" % t, "key%d" % t, N - t)
-            arrives("km%d" % t, "key%d" % t, N - t)
+            arrives("mark%d" % t, "key%d" % t, N - t)
 
+    part = {"A": (0, CUT // 16), "B": (CUT // 16, 16)}
     fill(T.ones[:], 1.0, ["ones"])
+    one = T.ones[:, 0:128]
     gp(lambda: g.iota(T.pi[:, 0:1], [[0, 1]], 0, 1), [], ["pi"])
     gp(lambda: g.iota(T.i16[:], [[1, 16]], 0, 0, allow_small_or_imprecise_dtypes=True), [], ["i16"])
-    gp(lambda: g.affine_select(T.eye[:], T.ones[:], [[-1, 128]], A.is_equal, 0.0, 0, 1), ["ones"], ["eye"])
-    gp(lambda: g.affine_select(T.c1[:], T.ones[:], [[-16, 8], [0, 16]], A.is_ge, 0.0, 0, 1), ["ones"], ["c1"])
+    gp(lambda: g.affine_select(T.eye[:], one, [[-1, 128]], A.is_equal, 0.0, 0, 1), ["ones"], ["eye"])
+    gp(lambda: g.affine_select(T.c1[:], one, [[-16, 8], [0, 16]], A.is_ge, 0.0, 0, 1), ["ones"], ["c1"])
     gp(lambda: g.affine_select(T.blk[:], T.c1[:], [[16, 8], [0, 16]], A.is_ge, 0.0, 15, -1), ["c1"], ["blk"])
     gp(lambda: g.affine_select(T.c3[:], T.blk[:], [[1, 128]], A.is_gt, 0.0, 0, -1), ["blk"], ["c3"])
     gp(lambda: g.iota(T.m1[:], [[0, 16], [1, 17]], -1, 0, allow_small_or_imprecise_dtypes=True), [], ["m1"])
-    fill(T.seed[:], 0.0, ["seed"])
-    act(T.seed[:, 0::17], T.ones[:, 0:16], F.Tanh, ["ones", "seed"], ["seed"], scale=16.0)
+    for s, (q0, q1) in part.items():
+        gp(lambda: g.iota(T["end" + s][:], [[16, q1 - q0], [0, 17 if s == "A" else WIDE]], 16 * q0 + 1, 0,
+                          allow_small_or_imprecise_dtypes=True), [], ["end" + s])
+    act(T.tsum[:], T.ones[:, 0:16], F.Tanh, ["ones"], ["ts%d" % j for j in range(16)], scale=0.0)
+    fill(T.junk[:, :, 0:128], float(R), ["junk%d" % j for j in range(16)])
     fill(T.slide[:], 0.0, ["slide"])
     fill(T.zero[:], 0.0, ["zero"])
+    fill(T.first[:, :, 0], 0.0, ["first_0"])
+    fill(T.mrow[:, :, 0], 0.0, ["mrow_0"])
+    fill(T.tab[:, 2 * V:], 0.0, ["spare"])
     ts(T.pj[:, 0:1], T.pi[:, 0:1], 15, A.bitwise_and, ["pi"], ["pj"])
-    fill(T.tsum[:], 0.0, ["ts%d" % j for j in range(16)])
     cp(T.cols[:, 0:1], T.pj[:, 0:1], ["pj"], ["c_pl"])
     ts(T.cols[:, 1:2], T.pj[:, 0:1], -37.0, A.mult, ["pj"], ["c_fb"], -37 * 18.5, A.add)
     ts(T.own[:], T.i16[:], T.cols[:, 0:1], A.is_equal, ["i16", "c_pl"], ["own"])
-    ts(T.lane[:], T.i16[:], 16.0, A.mult, ["i16", "c_pl"], ["lane"], T.cols[:, 0:1], A.add)
-    fill(T.first[:, :, 0], 0.0, ["first_0"])
-    ts(T.hi[:], T.own[:], 1.0 / 64, A.mult, ["own"], ["hi"])
-    ts(T.lo[:], T.own[:], -1.0, A.add, ["own"], ["lo"], 1.0 / 64, A.mult)
-    fill(T.mrow[:, :, 0], 0.0, ["mrow_0"])
-    ts(T.laneq[:], T.lane[:], 1.0 / R, A.mult, ["lane"], ["laneq"])
-    fill(T.tab[:, 2 * V:], 0.0, ["spare"])
-    ts(T.inbox[:, 0, 0:16], T.k0i[:], -2048.0, A.add, ["k0i"], ["key0"])
-    cp(T.inbox[:, 0, 16:32], T.k0i[:], ["k0i"], ["km0"])
+    ts(T.hi[:], T.own[:], 64.0, A.mult, ["own"], ["hi"])
+    ts(T.lo[:], T.own[:], -1.0, A.add, ["own"], ["lo"], 64.0, A.mult)
+    ts(T.inbox[:, 0, 0:16], T.k0i[:], -2048.0, A.add, ["k0i"], ["key0"], 1.0 / R, A.mult)
+    ts(T.inbox[:, 0, 16:32], T.k0i[:], 1.0 / R, A.mult, ["k0i"], ["mark0"])
     if r > 0:
-        send(0, T.inbox[:, N - r, :], T.inbox[:, 0, :], "key%d" % (N - r), True, ["key0", "km0"])
-    act(T.c2[:], T.eye[:], F.Identity, ["eye"], ["c2"], scale=-2.0)
-    act(T.eyem[:], T.eye[:], F.Identity, ["eye"], ["eyem"], scale=18.5)
-    act(T.eyeu[:], T.eye[:], F.Identity, ["eye"], ["eyeu"], scale=160.0)
-    act(T.eyef[:], T.eye[:], F.Copy, ["eye"], ["eyef"])
-    act(T.blku[:], T.blk[:], F.Identity, ["blk"], ["blku"], scale=-64.0)
-    act(T.blkd[:], T.blk[:], F.Identity, ["blk"], ["blkd"], scale=-1.0)
+        send(0, T.inbox[:, N - r, :], T.inbox[:, 0, :], "key%d" % (N - r), True, ["key0", "mark0"])
+    gp(lambda: g.affine_select(T.sel[:], T.junk[:, :, 0:128], [[-1, 16], [-16, 8], [0, 16]], A.is_equal, 0.0, 0, 1),
+       ["junk%d" % j for j in range(16)], ["sel"])
+    for name, src, c in (("c2", "eye", -2.0), ("eyem", "eye", 18.5), ("eyeu", "eye", 160.0),
+                         ("blku", "blk", -64.0), ("blkd", "blk", -1.0)):
+        act(T[name][:], T[src][:], F.Identity, [src], [name], scale=c)
     tt(T.c1[:], T.blk[:], T.c2[:], A.add, ["blk", "c2"], ["c1"])
     tt(T.low[:], T.eye[:], T.c3[:], A.subtract, ["eye", "c3"], ["low"])
-    ts(T.xm[:], T.c1[:], 1.0 / 64, A.mult, ["c1"], ["xm"])
+    ts(T.xm[:], T.c1[:], 64.0, A.mult, ["c1"], ["xm"])
     for i in range(16):
         if i < 10:
             cp(T.ax0[:, i::16], T.atom[:], ["atom"], ["ax0_%d" % i])
@@ -209,217 +217,265 @@ def rank_program(g, core, T, topo):
             act(T.ax0[:, i::16], T.atom[:], F.Copy, ["atom"], ["ax0_%d" % i])
     ax0 = ["ax0_%d" % i for i in range(16)]
     ts(T.slide[:, 15:143:16], T.blk[:, 0::16], 2.0, A.mult, ["blk", "slide"], ["slide"])
-    if MODES.count("P") < len(MODES):
-        act(T.sliden[:], T.slide[:], F.Identity, ["slide"], ["sliden"], scale=-0.5)
+    act(T.sliden[:], T.slide[:], F.Identity, ["slide"], ["sliden"], scale=-0.5)
     ts(T.cols[:, 2:3], T.thi[:, 0:1], -1.0, A.mult, ["thi"], ["c_th"], -941.5, A.add)
     cp(T.cols[:, 3:4], T.wi[:, 0:1], ["wi"], ["c_w"])
     ts(T.eyed[:], T.eye[:], 941.0, A.mult, ["eye"], ["eyed"])
     ts(T.ownr[:], T.m1[:], T.cols[:, 0:1], A.is_equal, ["m1", "c_pl"], ["ownr"])
-    ts(T.slidew[:], T.slide[:], T.cols[:, 3:4], A.mult, ["slide", "c_w"], ["slidew"], 0.5, A.mult)
+    ts(T.slidew[:], T.slide[:], T.cols[:, 3:4], A.mult, ["slide", "c_w"], ["slidew"], 0.5 / R, A.mult)
+    ts(T.eyeh[:], T.eye[:], -1023.5 / R, A.mult, ["eye"], ["eyeh"])
+    for s in part:
+        ts(T["cap" + s][:], T["end" + s][:], T.cols[:, 0:1], A.add, ["end" + s, "c_pl"] + ["endB%d" % j for j in range(4)],
+           ["cap" + s], 1.0 / R, A.mult)
     act(T.c4[:], T.c1[:], F.Identity, ["c1"], ["c4"], scale=5 * 18.5)
     act(T.c5[:], T.low[:], F.Identity, ["low"], ["c5"], scale=4 * 18.5)
+    act(T.tab[:, V:2 * V], T.chi[:], F.Copy, ["chi", "spare"], ["tab", "tabA", "tabB"])
+    tt(T.maskt[:], T.c4[:], T.c5[:], A.add, ["c4", "c5"], ["maskt"])
     for il in range(16):
-        act(T.sel[:, il, :], T.blk[:], F.Identity, ["blk", "own"], ["sel%d" % il], scale=T.own[:, il:il + 1])
         ts(T.seld[:, il, :], T.xm[:], T.lo[:, il:il + 1], A.max, ["xm", "lo", "hi"], ["seld%d" % il],
            T.hi[:, il:il + 1], A.min)
-    tt(T.maskt[:], T.c4[:], T.c5[:], A.add, ["c4", "c5"], ["maskt"])
-    cp(T.tab[:, V:2 * V], T.chi[:], ["chi"], ["tab"])
-    act(T.tab[:, 0:V], T.tab[:, V:2 * V], F.Copy, ["tab"], ["ch0"])
+    if r > 0:
+        dma("s", "l_c0", T.tab[:, 0:V], T.tab[:, V:2 * V], ["tab", "recs"], ["ch0"])
     wait("gp", [writer["recs"]])
     for k in range(1, N):
         send((r + k) % N, T["ax%d" % k][:], T.ax0[:], "tile%d" % k, False, ax0)
 
-    table = T.tab[:, V:2 * V + L]
-    edges = [0]
-    for n in CHUNKS:
-        edges.append(edges[-1] + n)
+    table = T.tab[:, V:2 * V + L + 8]
 
-    def lists(t):
-        slot = t if r > 0 else t % N
-        both = t == 0 or r == 0
-        w0, c0 = (32 if both else 16), 32 * t
-        src = ["key%d" % slot] + (["km%d" % slot] if both else [])
-        ts(T.lu[:, c0:c0 + w0], T.inbox[:, slot, 0:w0], 2048.0, A.add, src, ["luk%d" % t] + (["lum%d" % t] if both else []))
-        cp(T.lh[:, c0:c0 + w0], T.inbox[:, slot, 0:w0], src, ["lhk%d" % t] + (["lhm%d" % t] if both else []))
+    def stages(l0, l1):
+        return [s for s in STAGES if STAGES[s][0] < l1 and STAGES[s][1] > l0]
+
+    def slot_of(t):
+        return t if r > 0 else t % N
+
+    def offsets(t):
+        ts(T.lu[:, 32 * t:32 * t + 16], T.inbox[:, slot_of(t), 0:16], float(R), A.mult, ["key%d" % slot_of(t)],
+           ["luk%d" % t], 2048.0, A.add)
 
     def rows(lst, name):
-        mm(T.pu[:, L:2 * L], T.eye[:], T.zero[:], True, False, ["eye", "zero"], ["pu:r"])
+        mm(T.pr[:, 0:L], T.eye[:], T.zero[:], True, False, ["eye", "zero"], ["pr:r", "pr:open"])
         for il in range(16):
-            mm(T.pu[:, L + il:2 * L:16], T.sel[:, il, :], lst, False, il == 15, ["sel%d" % il, name], ["pu:r"])
+            mm(T.pr[:, il:L:16], T.sel[:, il, :], lst, False, il == 15, ["sel", name], ["pr:r", "pr:open"])
 
-    def weave(*chains):
-        chains = list(chains)
-        while chains:
-            chains = [c for c in chains if next(c, 0) is None]
-
+    offsets(0)
     for t in range(ROUNDS):
         last = t == ROUNDS - 1
-        out_keys = last or r < N - 1
-        slot = t if r > 0 else t % N
-        kn, mn = "key%d" % slot, "km%d" % slot
-        luk, lum, lhk, lhm = ["%s%d" % (x, t) for x in ("luk", "lum", "lhk", "lhm")]
-        keyp, km = T.inbox[:, slot, 0:16], T.inbox[:, slot, 16:32]
+        passes_on = last or r < N - 1
+        slot = slot_of(t)
+        kn, mn, luk, lum, on = "key%d" % slot, "mark%d" % slot, "luk%d" % t, "lum%d" % t, "out%d" % t
+        kq, km = T.inbox[:, slot, 0:16], T.inbox[:, slot, 16:32]
         c0 = 32 * t
         ax, axn = T["ax%d" % (t % N)], (ax0 if t % N == 0 else ["ax%d" % (t % N)])
-        both = t == 0 or r == 0
-        on = "out%d" % t
+        plain = t == 0 or r == 0
 
-        lists(t)
-        cp(T.cand[:], table.indirect(T.lu[:, c0:c0 + 16]), ["tab", "spare", luk], ["cand"])
-        act(T.tb[:], keyp, F.Identity, [kn], ["tb"], scale=-8.0, bias=1280 + 1.0 / 512)
-        act(T.kq[:], keyp, F.Identity, [kn], ["kq"], scale=1.0 / R)
-        mm(T.pq[:, 0:272], T.maskt[:], T.ownr[:], True, False, ["maskt", "ownr"], ["pq"])
-        for il in range(16):
-            mm(T.pq[:, 1 + il:272:17], T.seld[:, il, :], T.lh[:, c0:c0 + 16], False, False, ["seld%d" % il, lhk], ["pq"])
+        def cands(c):
+            l0, l1 = CANDS[c]
+            cp(T.cand[:, l0:l1], table.indirect(T.lu[:, c0 + l0 // 16:c0 + l1 // 16]), ["tabA", "tabB", luk],
+               ["cand%d" % q for q in range(l0 // 16, l1 // 16)])
+
+        def small(w):
+            if w == "ku" and not last:
+                offsets(t + 1)
+            elif w == "kmu" and not plain:
+                ts(T.lu[:, c0 + 16:c0 + 32], km, float(R), A.mult, [mn], [lum], 2048.0, A.add)
+            elif w == "tb":
+                act(T.tb[:], kq, F.Identity, [kn], ["tb"], scale=-8.0 * R, bias=1280 + 1.0 / 512)
+            elif w == "kx":
+                act(T.kx[:], kq, F.Identity, [kn], ["kx"], scale=float(R), bias=-160.0)
+            elif w == "um" and passes_on:
+                act(T.um[:], km, F.Relu, [mn], ["um"], scale=float(R), bias=0.5)
 
         def marks():
-            if not both:
-                cp(T.lh[:, c0 + 16:c0 + 32], km, [mn], [lhm])
-                ts(T.lu[:, c0 + 16:c0 + 32], km, 2048.0, A.add, [mn], [lum])
-            rows(T.lh[:, c0 + 16:c0 + 32], lhm)
-            act(T.mrow[:, :, 1:17], T.pu[:, L:2 * L], F.Sign, ["pu:r"], ["mrow"], bias=0.5)
-            act(T.vrow[:], T.pu[:, L:2 * L], F.Copy, ["pu:r"], ["vrow"])
-            mm(T.pq[:, 0:272], T.eyem[:], T.mrow[:], False, False, ["eyem", "mrow", "mrow_0"], ["pq"])
+            rows(km, mn)
+            yield
+            act(T.mrow[:, :, 1:17], T.pr[:, 0:L], F.Sign, ["pr:r"], ["mrow"], bias=0.5)
+            yield
+            act(T.vrow[:], T.pr[:, 0:L], F.Copy, ["pr:r"], ["vrow"])
 
-        def base():
-            act(T.basef[:], T.tab[:, 0:2 * V].indirect(T.lu[:, c0 + 16:c0 + 32]), F.Copy, ["tab", "ch0", lum], ["base"])
+        def near(s):
+            q0, q1 = part[s]
+            pq, on = T["pq" + s], ["pq" + s]
+            mm(pq[:, 17 * q0:17 * q1], T.maskt[:], T.ownr[:, 17 * q0:17 * q1], True, False, ["maskt", "ownr"], on)
+            for il in range(16):
+                mm(pq[:, 17 * q0 + 1 + il:17 * q1:17], T.seld[:, il, :], T.inbox[:, slot, q0:q1], False, False,
+                   ["seld%d" % il, kn], on)
+            yield
+            mm(pq[:, 17 * q0:17 * q1], T.eyem[:], T.mrow[:, q0:q1], False, False, ["eyem", "mrow", "mrow_0"], on)
 
         def gather(c):
-            l0, l1 = edges[c], edges[c + 1]
+            l0, l1, mode = PIECES[c]
             out, x = T.diff[:, 16 * l0:16 * l1], T.recs[:].indirect(T.cand[:, l0:l1])
-            if MODES[c] == "R":
-                act(out, x, F.Copy, ["recs", "cand"], ["diff%d" % c])
+            cn = ["cand%d" % q for q in range(l0 // 16, l1 // 16)]
+            if mode == "R":
+                act(out, x, F.Copy, ["recs"] + cn, ["diff%d" % c])
             else:
-                tt(out, x, ax[:, 16 * l0:16 * l1], A.subtract, ["recs", "cand"] + axn, ["diff%d" % c])
+                tt(out, x, ax[:, 16 * l0:16 * l1], A.subtract, ["recs"] + cn + axn, ["diff%d" % c])
 
         def absval(c):
-            l0, l1 = edges[c], edges[c + 1]
+            l0, l1, mode = PIECES[c]
             out, x = T.absd[:, 16 * l0:16 * l1], T.diff[:, 16 * l0:16 * l1]
-            if MODES[c] == "R":
+            if mode == "R":
                 tt(out, x, ax[:, 16 * l0:16 * l1], A.max, ["diff%d" % c] + axn, ["abs%d" % c])
-            elif MODES[c] == "Q":
+            elif mode == "Q":
                 ts(out, x, 0.0, A.max, ["diff%d" % c], ["abs%d" % c])
             else:
                 act(out, x, F.Abs, ["diff%d" % c], ["abs%d" % c], scale=0.5)
 
-        def negs(s):
-            mm(T.pd[:, s, 0:64], T.eyed[:], T.ones[:, 0:64], True, False, ["eyed", "ones"], ["pd%d" % s])
-            cs = [c for c in range(len(CHUNKS)) if edges[c] // 64 == s and MODES[c] != "P"]
-            if cs:
-                l0, l1 = edges[cs[0]], edges[cs[-1] + 1]
-                o = T.pd[:, s, l0 - 64 * s:l1 - 64 * s]
-                if MODES[cs[0]] == "R":
-                    mm(o, T.blkd[:], ax[:, 16 * l0:16 * l1:16], False, False, ["blkd"] + axn, ["pd%d" % s])
-                for i in range(16):
-                    mm(o, T.sliden[:, 15 - i:143 - i], T.diff[:, 16 * l0 + i:16 * l1:16], False, False,
-                       ["sliden"] + ["diff%d" % c for c in cs], ["pd%d" % s])
+        def pieces(b, modes):
+            cs = [c for c in range(len(PIECES)) if SUMS[b][0] <= PIECES[c][0] < SUMS[b][1] and PIECES[c][2] in modes]
+            return (cs, min(PIECES[c][0] for c in cs), max(PIECES[c][1] for c in cs)) if cs else ([], 0, 0)
 
-        def sums(s):
-            l0, l1 = 64 * s, 64 * s + 64
-            src = ["abs%d" % c for c in range(len(CHUNKS)) if edges[c] < l1 and edges[c + 1] > l0]
+        def linear(b):
+            l0, l1 = SUMS[b]
+            s = stages(l0, l1)[0]
+            out, on = T["pd" + s], ["pd%s:%d" % (s, b)]
+            mm(out[:, l0:l1], T.eyed[:], T.ones[:, l0:l1], True, False, ["eyed", "ones"], on + ["pd%s:open" % s])
+            rs, n0, n1 = pieces(b, "R")
+            if rs:
+                mm(out[:, n0:n1], T.blkd[:], ax[:, 16 * n0:16 * n1:16], False, False, ["blkd"] + axn, on)
+            cs, n0, n1 = pieces(b, "QR")
+            for i in range(16 if cs else 0):
+                mm(out[:, n0:n1], T.sliden[:, 15 - i:143 - i], T.diff[:, 16 * n0 + i:16 * n1:16], False, False,
+                   ["sliden"] + ["diff%d" % c for c in cs], on)
+
+        def sums(b):
+            l0, l1 = SUMS[b]
+            s = stages(l0, l1)[0]
             for i in range(16):
-                mm(T.pd[:, s, 0:64], T.slide[:, 15 - i:143 - i], T.absd[:, 16 * l0 + i:16 * l1:16], False, i == 15,
-                   ["slide"] + src, ["pd%d" % s])
+                mm(T["pd" + s][:, l0:l1], T.slide[:, 15 - i:143 - i], T.absd[:, 16 * l0 + i:16 * l1:16], False, i == 15,
+                   ["slide"] + ["abs%d" % c for c in pieces(b, "PQR")[0]], ["pd%s:%d" % (s, b), "pd%s:open" % s])
 
-        def fails(s):
-            l0, l1 = 64 * s, 64 * s + 64
-            act(T.sgn[:, l0:l1], T.pd[:, s, 0:64], F.Sign, ["pd%d" % s, "c_th"], ["sgn%d" % s], bias=T.cols[:, 2:3])
-            mm(T.pz[:, l0:l1], T.eyem[:], T.mrow[:, 4 * s:4 * s + 4, 1:17], True, False, ["eyem", "mrow"], ["pz:%d" % s])
-            mm(T.pz[:, l0:l1], T.low[:], T.sgn[:, l0:l1], False, True, ["low", "sgn%d" % s], ["pz:%d" % s])
+        def staged(w, s):
+            l0, l1 = STAGES[s]
+            q0, q1 = l0 // 16, l1 // 16
+            d, dn = T["pd" + s][:, l0:l1], ["pd%s:%d" % (s, b) for b in range(len(SUMS)) if l0 <= SUMS[b][0] < l1]
+            fs, ms = T.first[:, q0:q1, 1:17], T.mrow[:, q0:q1, 1:17]
+            u, un = (T.pu[:, l0:l1], ["pu:" + s, "pu:open"]) if l0 < CUT else (T.pr[:, L + l0:L + l1], ["pr:" + s, "pr:open"])
+            if w == "sg":
+                act(T.sgn[:, l0:l1], d, F.Sign, dn + ["c_th"], ["sgn" + s], bias=T.cols[:, 2:3])
+                yield
+                mm(T.pz[:, l0:l1], T.eyem[:], ms, True, False, ["eyem", "mrow"], ["pz:" + s])
+                mm(T.pz[:, l0:l1], T.low[:], T.sgn[:, l0:l1], False, True, ["low", "sgn" + s], ["pz:" + s])
+            elif w == "u":
+                mm(u, T.eye[:], T.vrow[:, l0:l1], True, False, ["eye", "vrow"], un)
+                mm(u, T.eyeu[:], ms, False, False, ["eyeu", "mrow"], un)
+            elif w == "fi":
+                act(fs, T.pz[:, l0:l1], F.Relu, ["pz:" + s, "c_fb"], ["first" + s], scale=37.0, bias=T.cols[:, 1:2])
+                yield
+                mm(u, T.blku[:], fs, False, True, ["blku", "first" + s], un)
+                yield
+                h = "A" if l0 < CUT else "B"
+                mm(T["pq" + h][:, 17 * q0:17 * q1], T.blkd[:], T.first[:, q0:q1, :], False, q1 == part[h][1],
+                   ["blkd", "first" + s, "first_0"], ["pq" + h])
+            elif w == "dh":
+                if passes_on and s in DH_SCALAR:
+                    act(T.dh[:, l0:l1], d, F.Identity, dn, ["dh" + s], bias=-2989.0)
+                elif passes_on:
+                    ts(T.dh[:, l0:l1], d, -2989.0, A.add, dn, ["dh" + s])
+            elif w == "xi":
+                tt(T.xi[:, l0:l1], d, fs, A.mult, dn + ["first" + s], ["xi" + s])
 
-        def first(s):
-            l0, l1 = 64 * s, 64 * s + 64
-            fs = T.first[:, 4 * s:4 * s + 4, 1:17]
-            act(fs, T.pz[:, l0:l1], F.Relu, ["pz:%d" % s, "c_fb"], ["first%d" % s], scale=37.0, bias=T.cols[:, 1:2])
-            mm(T.pu[:, l0:l1], T.eyef[:], T.vrow[:, l0:l1], True, False, ["eyef", "vrow"], ["pu:%d" % s])
-            mm(T.pu[:, l0:l1], T.eyeu[:], T.mrow[:, 4 * s:4 * s + 4, 1:17], False, False, ["eyeu", "mrow"], ["pu:%d" % s])
-            mm(T.pq[:, 68 * s:68 * s + 68], T.blkd[:], T.first[:, 4 * s:4 * s + 4, :], False, s == 3,
-               ["blkd", "first%d" % s, "first_0"], ["pq"])
-            mm(T.pu[:, l0:l1], T.blku[:], fs, False, True, ["blku", "first%d" % s], ["pu:%d" % s])
+        def far(j):
+            n = min(16 * j, CUT)
+            act(T.junk[:, j, 0:n], T.pu[:, 0:n], F.Tanh, ["pu:" + s for s in stages(0, n)] + ["tb"],
+                ["junk%d" % j, "ts%d" % j], scale=8.0, bias=T.tb[:, j:j + 1], accum_out=T.tsum[:, j:j + 1])
 
-        def rivals(j):
-            src = ["pu:%d" % s for s in range(4) if 64 * s < 16 * j]
-            act(T.junk[:, j, 0:16 * j], T.pu[:, 0:16 * j], F.Tanh, src + ["tb"], ["junk%d" % j, "ts%d" % j],
-                scale=8.0, bias=T.tb[:, j:j + 1], accum_out=T.tsum[:, j:j + 1])
+        def late(j):
+            ts(T.hitB[:, j - CUT // 16, 17:17 + 16 * j - CUT], T.pr[:, L + CUT:L + 16 * j], T.kx[:, j:j + 1], A.is_equal,
+               ["pr:" + s for s in stages(CUT, 16 * j)] + ["kx"], ["hit%d" % j])
 
-        def mend(s0, s1):
-            l0, l1 = 64 * s0, 64 * s1 + 64
-            ss = range(s0, s1 + 1)
-            yield tt(T.xi[:, l0:l1], T.pd[:, s0:s1 + 1, 0:64], T.first[:, 4 * s0:4 * s1 + 4, 1:17], A.mult,
-                     ["pd%d" % s for s in ss] + ["first%d" % s for s in ss], ["xi%d" % s0])
-            yield ts(T.ei[:, l0:l1], T.xi[:, l0:l1], 2047, A.bitwise_and, ["xi%d" % s0], ["ei%d" % s0])
-            yield tt(T.si[:, l0:l1], T.ei[:, l0:l1], T.basef[:, l0:l1], A.add, ["ei%d" % s0, "base"], ["si%d" % s0])
-            yield ts(T.col[:, l0:l1], T.si[:, l0:l1], R - 1, A.bitwise_and, ["si%d" % s0], ["col%d" % s for s in ss])
+        def counted(s):
+            q0, q1 = part[s]
+            ts(T.ti[:, q0:q1], T.tsum[:, q0:q1], 512.0, A.mult, ["ts%d" % j for j in range(q0, q1)], ["ti" + s])
+            yield
+            ts(T.zi[:, q0:q1], T.ti[:, q0:q1], 511, A.bitwise_and, ["ti" + s], ["zi" + s])
+            yield
+            tt(T.capA[:, 0::17] if s == "A" else T.capB[:, :, 0], T.zi[:, q0:q1], T.inbox[:, slot, q0:q1], A.add, ["zi" + s, kn], ["cap" + s])
 
-        def half(s0, s1):
-            if out_keys:
-                ts(T.dh[:, 64 * s0:64 * s1 + 64], T.pd[:, s0:s1 + 1, 0:64], -2989.0, A.add,
-                   ["pd%d" % s for s in range(s0, s1 + 1)], ["dh%d" % s for s in range(s0, s1 + 1)])
+        def winners(s):
+            q0, q1 = part[s]
+            hit = T.hitA[:] if s == "A" else T.hitB[:, :, 0:17]
+            ts(hit, T["pq" + s][:, 17 * q0:17 * q1], 0.0, A.is_equal, ["pq" + s], ["hit" + s])
+            yield
+            if s == "A":
+                op("v", lambda: v.tensor_tensor_scan(T.endA[:], T.hitA[:], T.capA[:], 0.0, A.add, A.min),
+                   ["hitA", "capA"], ["endA"])
+                end, en = T.endA[:, 16::17], ["endA"]
+            else:
+                for j in range(q1 - q0):
+                    n = 17 + 16 * j
+                    op("v", lambda: v.tensor_tensor_scan(T.endB[:, j, WIDE - n:WIDE], T.hitB[:, j, 0:n], T.capB[:, j, 0:n],
+                                                         0.0, A.add, A.min),
+                       ["hitB", "capB", "hit%d" % (q0 + j)], ["endB%d" % j])
+                end, en = T.endB[:, :, WIDE - 1], ["endB%d" % j for j in range(q1 - q0)]
+            yield
+            ts(T.ou[:, q0:q1], end, float(R), A.mult, en, ["ou" + s], 2048.0, A.add)
 
-        def key_sums():
-            if out_keys:
-                for jl in range(16):
-                    mm(T.pk[:, 0:16], T.slidew[:, 15 - jl:143 - jl], T.dh[:, jl::16], jl == 0, jl == 15,
-                       ["slidew", "dh0", "dh1", "dh2", "dh3"], ["pk"])
+        def mend(s):
+            l0, l1 = MENDS[s]
+            ts(T.ei[:, l0:l1], T.xi[:, l0:l1], 2047, A.bitwise_and, ["xi" + x for x in stages(l0, l1)], ["ei" + s])
+            yield
+            if plain:
+                base, rd = table.indirect(T.lu[:, c0 + l0 // 16:c0 + l1 // 16]), [luk]
+            else:
+                base, rd = T.tab[:, 0:2 * V].indirect(T.lu[:, c0 + 16 + l0 // 16:c0 + 16 + l1 // 16]), ["ch0", lum]
+            tt(T.si[:, l0:l1], base, T.ei[:, l0:l1], A.add, rd + ["ei" + s, "tab" + s, "tab"], ["si" + s])
+            yield
+            ts(T.col[:, l0:l1], T.si[:, l0:l1], R - 1, A.bitwise_and, ["si" + s], ["col" + s])
 
         def keys():
-            if out_keys:
-                yield ts(T.k1[:], T.pk[:, 0:16], 524288.0, A.add, ["pk"], ["k1"])
-                yield ts(T.k2[:], T.k1[:], V - 1, A.bitwise_and, ["k1"], ["k2"])
-                yield ts(T.outbox[:, t, 0:16], T.k2[:], -2048.0, A.add, ["k2"], [on + "k"])
+            if passes_on:
+                o = T.pz[:, L:L + 16]
+                mm(o, T.eyeh[:], T.ones[:, 0:16], True, False, ["eyeh", "ones"], ["pz:k"])
+                for jl in range(16):
+                    mm(o, T.slidew[:, 15 - jl:143 - jl], T.dh[:, jl::16], False, jl == 15,
+                       ["slidew"] + ["dh" + s for s in STAGES], ["pz:k"])
+                yield
+                act(T.k1[:], o, F.Identity, ["pz:k"], ["k1"], bias=HALVES)
+                yield
+                ts(T.k2[:], T.k1[:], -HALVES, A.add, ["k1"], ["k2"], 1024.5 / R, A.add)
+                yield
+                tt(T.outbox[:, t, 0:16], o, T.k2[:], A.subtract, ["pz:k", "k2"], [on + "k"])
                 if not last:
                     send(r + 1, T.inbox[:, t + 1, 0:16], T.outbox[:, t, 0:16], "key%d" % (t + 1), True, [on + "k"])
 
-        def block():
-            yield op("v", lambda: v.tensor_tensor_scan(T.prod[:], T.pq[:, 0:272], T.seed[:], 0.0, A.mult, A.add),
-                     ["pq", "seed"], ["prod"])
-            yield ts(T.nw[:], T.prod[:, 16::17], 0.0, A.is_equal, ["prod"], ["nw"])
-            yield tt(T.o0[:], T.nw[:], T.kq[:], A.add, ["nw", "kq"], ["o0"])
-
-        def write():
-            ts(T.ti[:], T.tsum[:], 512.0, A.mult, ["ts%d" % j for j in range(16)], ["ti"])
-            ts(T.zi[:], T.ti[:], 511, A.bitwise_and, ["ti"], ["zi"])
-            tt(T.o1[:], T.o0[:], T.zi[:], A.add, ["o0", "zi"], ["o1"])
-            tt(T.o2[:], T.o1[:], T.laneq[:], A.min, ["o1", "laneq"], ["o2"])
-            if out_keys:
-                ts(T.lost[:], T.o2[:], 0.0, A.is_ge, ["o2"], ["lost"], 2048.0, A.mult)
-            ts(T.ou[:], T.o2[:], float(R), A.mult, ["o2"], ["ou"], 2048.0, A.add)
-            if out_keys:
+        def new_marks():
+            if passes_on:
+                ts(T.lost[:], T.ou[:], 2048.0, A.is_ge, ["ouA", "ouB"], ["lost"], 0.5, A.mult)
+                yield
                 tt(T.nm[:], T.lost[:], T.um[:], A.min, ["lost", "um"], ["nm"])
+                yield
                 if not last:
                     tt(T.outbox[:, t, 16:32], T.nm[:], T.outbox[:, t, 0:16], A.add, ["nm", on + "k"], [on + "m"])
                     send(r + 1, T.inbox[:, t + 1, 16:32], T.outbox[:, t, 16:32], "mark%d" % (t + 1), True, [on + "m"])
-            cp(table.indirect(T.ou[:]), T.col[:], ["ou"] + ["col%d" % s for s in range(4)], ["tab", "spare"])
 
-        for w in ORDER.split():
-            k, n = w[0], w[1:]
-            if w == "M":
-                marks()
-            elif w == "base":
-                base()
-            elif w == "um":
-                if out_keys:
-                    act(T.ums[:], km, F.Sign, [mn], ["ums"], bias=0.5)
-                    act(T.um[:], T.ums[:], F.Identity, ["ums"], ["um"], scale=1024.0, bias=1024.0)
-            elif w == "K":
-                key_sums()
-            elif w == "W":
-                write()
-            elif k == "m":
-                if n[1] == "3":
-                    weave(mend(int(n[0]), 3), block(), keys())
-                else:
-                    weave(mend(int(n[0]), int(n[1])))
-            elif k == "h":
-                half(int(n[0]), int(n[1]))
+        def step(w):
+            if w in ("ku", "kmu", "tb", "kx", "um"):
+                small(w)
+            elif w in ("M", "K", "nm"):
+                yield from {"M": marks, "K": keys, "nm": new_marks}[w]()
+            elif w[0] == "W":
+                q0, q1 = part[w[1]]
+                cp(table.indirect(T.ou[:, q0:q1]), T.col[:, 16 * q0:16 * q1], ["ou" + w[1], "col" + w[1]],
+                   ["tab" + w[1], "tab"])
+            elif w[-1] in "AB":
+                yield from {"q": near, "z": counted, "o": winners, "m": mend}[w[0]](w[1])
+            elif "." in w:
+                yield from staged(*w.split("."))
             else:
-                {"g": gather, "b": absval, "n": negs, "s": sums, "f": fails, "p": first, "r": rivals}[k](int(n))
+                {"c": cands, "g": gather, "b": absval, "l": linear, "s": sums, "r": far, "e": late}[w[0]](int(w[1:]))
 
-    dma("s", "st_c", T.yc[:], T.tab[:, V:2 * V], ["tab"], [])
-    tt(T.o1[:], T.outbox[:, ROUNDS - 1, 0:16], T.nm[:], A.subtract, ["out%dk" % (ROUNDS - 1), "nm"], ["o1"])
-    ts(T.vh[:], T.o1[:], 2048.0, A.add, ["o1"], ["vh"])
+        live = {}
+        for w in ORDER.split():
+            if w not in live:
+                live[w] = step(w)
+            next(live[w], None)
+
+    dma("s", "st_c", T.yc[:], T.tab[:, V:2 * V], ["tabA", "tabB"], [])
+    tt(T.lost[:], T.outbox[:, ROUNDS - 1, 0:16], T.nm[:], A.subtract, ["out%dk" % (ROUNDS - 1), "nm"], ["lost"])
+    ts(T.vh[:], T.lost[:], 0.5, A.add, ["lost"], ["vh"])
     rows(T.vh[:], "vh")
-    act(T.vrow[:], T.pu[:, L:2 * L], F.Identity, ["pu:r"], ["vrow"], bias=2048.0)
-    dma("a", "st_k", T.yk[:], T.vrow[0:128:16, :], ["vrow"], [])
+    act(T.krow[:], T.pr[:, 0:L], F.Identity, ["pr:r"], ["krow"], bias=2048.0)
+    dma("a", "st_k", T.yk[:], T.krow[0:128:16, :], ["krow"], [])
     g.wait_ge(T.sem.sent, sent[0])
     wait("gp", [(e, n) for e, n in count.items()] + [("st_c", 16), ("st_k", 16)])

@@ -2,25 +2,28 @@ from concourse.mybir import AluOpType as A, ActivationFunctionType as F
 
 V, R, L, ROUNDS, N = 2048, 4096, 256, 8, 4
 CUT = 192
-PIECES = ((0, 64, "R"), (64, 128, "P"), (128, 192, "R"), (192, 224, "Q"), (224, 256, "Q"))
+PIECES = ((0, 64, "P"), (64, 128, "R"), (128, 192, "P"), (192, 256, "Q"))
 SUMS = ((0, 64), (64, 128), (128, 192), (192, 256))
-CANDS = ((0, 64), (64, 256))
+CANDS = ((0, 128), (128, 256))
 STAGES = {"a": (0, 128), "b": (128, 192), "c": (192, 256)}
-MENDS = {"A": (0, 192), "B": (192, 256)}
-DH_SCALAR = ""
-ORDER = ("c0 kx c1 g0 qA g2 g1 kmu b0 qB M b2 l0 s0 l1 l2 b1 s2 M g3 sg.b g4 s1 M u.a sg.a sg.b dh.a sg.a fi.a b4 fi.a "
-         "fi.b u.b tb fi.b r13 b3 l3 r5 xi.b xi.a mA s3 r14 qA dh.b r12 r4 sg.c sg.c u.c r7 mA fi.c r2 dh.c fi.c xi.c "
-         "e13 r15 zB fi.a qB fi.b r8 K fi.c e15 r10 mA e14 mB oA r11 zB r6 r3 r1 r9 oB K mB zA zB K mB um zA oB zA K "
-         "oB oA WB oA nm WA nm ku nm")
+MENDS = {"A": (0, 128), "C": (128, 192), "B": (192, 256)}
+WRITES = {"A": (0, 8), "C": (8, 12), "B": (12, 16)}
+DH_SCALAR = "c"
+STEP_SCALAR = ""
+FIRST = 1.0 if STEP_SCALAR else 37.0
+ORDER = ("c0 qB g1 c1 g0 i.a g2 qA M l1 b0 b1 s0 g3 b3 b2 M kx s1 i.c sg.a i.b s2 sg.a tb M sg.b u.a fi.a qA xi.a sg.b "
+         "dh.a fi.b dh.b kmu fi.a u.b mA xi.b mA l3 r1 s3 r2 r3 u.c fi.a r7 r4 r6 r5 zA dh.c fi.b sg.c qB r8 r9 fi.b "
+         "mA sg.c fi.c fi.c fi.c zA r11 mC hA zA mC xi.c r10 oA r15 hB e14 r12 zC oA r13 mC K mB zC WA r14 zC K zB e15 "
+         "K zB oC K e13 zB mB oC oB WC oB mB nm um WB nm ku nm")
 HALVES = 1.5 * 2 ** 22
 WIDE = 1 + L - CUT
 
 SCRATCH = {n: ("sbuf", s, d) for d, s, names in (
     ("bfloat16", [128, R], "recs ax0 ax1 ax2 ax3 diff absd"),
-    ("bfloat16", [128, L], "atom sgn zero ones"),
+    ("bfloat16", [128, L], "atom sgn nb cd zero ones"),
     ("bfloat16", [128, 16, 17], "first mrow"),
     ("bfloat16", [128, 16, L], "junk"),
-    ("bfloat16", [128, 128], "c1 c2 c3 blk eye eyem eyeu low blku blkd xm"),
+    ("bfloat16", [128, 128], "c1 c2 c3 blk eye eyem eyeu eye37 eyen low blku blkd blk37 xm"),
     ("bfloat16", [128, 144], "slide sliden slidew"),
     ("bfloat16", [128, 16, 128], "sel seld"),
     ("bfloat16", [128, 272], "ownr m1"),
@@ -47,7 +50,7 @@ SCRATCH = {n: ("sbuf", s, d) for d, s, names in (
 ) for n in names.split()}
 BANKS = ("pda", "pdb", "pdc", "pz", "pu", "pr", "pqA", "pqB")
 SCRATCH.update({n: ("psum", [128, 512], "float32") for n in BANKS})
-SEMAPHORES = (["v", "a", "p", "gp", "l_at", "l_k0", "l_th", "l_w", "l_ch", "l_rec", "l_c0", "sent", "st_c", "st_k"]
+SEMAPHORES = (["v", "a", "p", "gp", "l_at", "l_k0", "l_th", "l_w", "l_ch", "l_rec", "sent", "st_c", "st_k"]
               + ["%s%d" % (x, t) for x in ("key", "mark") for t in range(1, ROUNDS)]
               + ["tile%d" % k for k in range(1, N)])
 
@@ -194,7 +197,7 @@ def rank_program(g, core, T, topo):
     fill(T.tab[:, 2 * V:], 0.0, ["spare"])
     ts(T.pj[:, 0:1], T.pi[:, 0:1], 15, A.bitwise_and, ["pi"], ["pj"])
     cp(T.cols[:, 0:1], T.pj[:, 0:1], ["pj"], ["c_pl"])
-    ts(T.cols[:, 1:2], T.pj[:, 0:1], -37.0, A.mult, ["pj"], ["c_fb"], -37 * 18.5, A.add)
+    ts(T.cols[:, 1:2], T.pj[:, 0:1], -FIRST, A.mult, ["pj"], ["c_fb"], -18.5 * FIRST, A.add)
     ts(T.own[:], T.i16[:], T.cols[:, 0:1], A.is_equal, ["i16", "c_pl"], ["own"])
     ts(T.hi[:], T.own[:], 64.0, A.mult, ["own"], ["hi"])
     ts(T.lo[:], T.own[:], -1.0, A.add, ["own"], ["lo"], 64.0, A.mult)
@@ -205,7 +208,8 @@ def rank_program(g, core, T, topo):
     gp(lambda: g.affine_select(T.sel[:], T.junk[:, :, 0:128], [[-1, 16], [-16, 8], [0, 16]], A.is_equal, 0.0, 0, 1),
        ["junk%d" % j for j in range(16)], ["sel"])
     for name, src, c in (("c2", "eye", -2.0), ("eyem", "eye", 18.5), ("eyeu", "eye", 160.0),
-                         ("blku", "blk", -64.0), ("blkd", "blk", -1.0)):
+                         ("eye37", "eye", 37.0), ("eyen", "eye", -2048.0), ("blku", "blk", -64.0 * 37 / FIRST),
+                         ("blkd", "blk", -1.0), ("blk37", "blk", -37.0 / FIRST)):
         act(T[name][:], T[src][:], F.Identity, [src], [name], scale=c)
     tt(T.c1[:], T.blk[:], T.c2[:], A.add, ["blk", "c2"], ["c1"])
     tt(T.low[:], T.eye[:], T.c3[:], A.subtract, ["eye", "c3"], ["low"])
@@ -224,18 +228,19 @@ def rank_program(g, core, T, topo):
     ts(T.ownr[:], T.m1[:], T.cols[:, 0:1], A.is_equal, ["m1", "c_pl"], ["ownr"])
     ts(T.slidew[:], T.slide[:], T.cols[:, 3:4], A.mult, ["slide", "c_w"], ["slidew"], 0.5 / R, A.mult)
     ts(T.eyeh[:], T.eye[:], -1023.5 / R, A.mult, ["eye"], ["eyeh"])
+    ts(T.cols[:, 5:6], T.own[:, 0:1], 166.0 * 2048, A.mult, ["own"], ["c_cd"], T.own[:, 1:2], A.add)
+    act(T.cd[:], T.ones[:], F.Identity, ["ones", "c_cd"], ["cd"], scale=T.cols[:, 5:6])
     for s in part:
-        ts(T["cap" + s][:], T["end" + s][:], T.cols[:, 0:1], A.add, ["end" + s, "c_pl"] + ["endB%d" % j for j in range(4)],
-           ["cap" + s], 1.0 / R, A.mult)
+        ts(T["cap" + s][:], T["end" + s][:], T.cols[:, 0:1], A.add, ["endA", "endB", "endC", "endD", "c_pl"] + ["endB%d" % j for j in range(4)],
+           ["cap" + x for x in WRITES if (x == "B") == (s == "B")], 1.0 / R, A.mult)
     act(T.c4[:], T.c1[:], F.Identity, ["c1"], ["c4"], scale=5 * 18.5)
     act(T.c5[:], T.low[:], F.Identity, ["low"], ["c5"], scale=4 * 18.5)
-    act(T.tab[:, V:2 * V], T.chi[:], F.Copy, ["chi", "spare"], ["tab", "tabA", "tabB"])
+    tabs = ["tab" + s for s in WRITES]
+    act(T.tab[:, V:2 * V], T.chi[:], F.Copy, ["chi", "spare"], ["tab"] + tabs)
     tt(T.maskt[:], T.c4[:], T.c5[:], A.add, ["c4", "c5"], ["maskt"])
     for il in range(16):
         ts(T.seld[:, il, :], T.xm[:], T.lo[:, il:il + 1], A.max, ["xm", "lo", "hi"], ["seld%d" % il],
            T.hi[:, il:il + 1], A.min)
-    if r > 0:
-        dma("s", "l_c0", T.tab[:, 0:V], T.tab[:, V:2 * V], ["tab", "recs"], ["ch0"])
     wait("gp", [writer["recs"]])
     for k in range(1, N):
         send((r + k) % N, T["ax%d" % k][:], T.ax0[:], "tile%d" % k, False, ax0)
@@ -267,10 +272,11 @@ def rank_program(g, core, T, topo):
         c0 = 32 * t
         ax, axn = T["ax%d" % (t % N)], (ax0 if t % N == 0 else ["ax%d" % (t % N)])
         plain = t == 0 or r == 0
+        left = {}
 
         def cands(c):
             l0, l1 = CANDS[c]
-            cp(T.cand[:, l0:l1], table.indirect(T.lu[:, c0 + l0 // 16:c0 + l1 // 16]), ["tabA", "tabB", luk],
+            cp(T.cand[:, l0:l1], table.indirect(T.lu[:, c0 + l0 // 16:c0 + l1 // 16]), tabs + [luk],
                ["cand%d" % q for q in range(l0 // 16, l1 // 16)])
 
         def small(w):
@@ -329,7 +335,6 @@ def rank_program(g, core, T, topo):
             l0, l1 = SUMS[b]
             s = stages(l0, l1)[0]
             out, on = T["pd" + s], ["pd%s:%d" % (s, b)]
-            mm(out[:, l0:l1], T.eyed[:], T.ones[:, l0:l1], True, False, ["eyed", "ones"], on + ["pd%s:open" % s])
             rs, n0, n1 = pieces(b, "R")
             if rs:
                 mm(out[:, n0:n1], T.blkd[:], ax[:, 16 * n0:16 * n1:16], False, False, ["blkd"] + axn, on)
@@ -341,9 +346,10 @@ def rank_program(g, core, T, topo):
         def sums(b):
             l0, l1 = SUMS[b]
             s = stages(l0, l1)[0]
+            left[s] -= l1 - l0
             for i in range(16):
-                mm(T["pd" + s][:, l0:l1], T.slide[:, 15 - i:143 - i], T.absd[:, 16 * l0 + i:16 * l1:16], False, i == 15,
-                   ["slide"] + ["abs%d" % c for c in pieces(b, "PQR")[0]], ["pd%s:%d" % (s, b), "pd%s:open" % s])
+                mm(T["pd" + s][:, l0:l1], T.slide[:, 15 - i:143 - i], T.absd[:, 16 * l0 + i:16 * l1:16], False,
+                   i == 15 and left[s] == 0, ["slide"] + ["abs%d" % c for c in pieces(b, "PQR")[0]], ["pd%s:%d" % (s, b)])
 
         def staged(w, s):
             l0, l1 = STAGES[s]
@@ -351,7 +357,10 @@ def rank_program(g, core, T, topo):
             d, dn = T["pd" + s][:, l0:l1], ["pd%s:%d" % (s, b) for b in range(len(SUMS)) if l0 <= SUMS[b][0] < l1]
             fs, ms = T.first[:, q0:q1, 1:17], T.mrow[:, q0:q1, 1:17]
             u, un = (T.pu[:, l0:l1], ["pu:" + s, "pu:open"]) if l0 < CUT else (T.pr[:, L + l0:L + l1], ["pr:" + s, "pr:open"])
-            if w == "sg":
+            if w == "i":
+                left[s] = l1 - l0
+                mm(d, T.eyed[:], T.ones[:, l0:l1], True, False, ["eyed", "ones"], dn + ["pd%s:e" % s])
+            elif w == "sg":
                 act(T.sgn[:, l0:l1], d, F.Sign, dn + ["c_th"], ["sgn" + s], bias=T.cols[:, 2:3])
                 yield
                 mm(T.pz[:, l0:l1], T.eyem[:], ms, True, False, ["eyem", "mrow"], ["pz:" + s])
@@ -360,20 +369,31 @@ def rank_program(g, core, T, topo):
                 mm(u, T.eye[:], T.vrow[:, l0:l1], True, False, ["eye", "vrow"], un)
                 mm(u, T.eyeu[:], ms, False, False, ["eyeu", "mrow"], un)
             elif w == "fi":
-                act(fs, T.pz[:, l0:l1], F.Relu, ["pz:" + s, "c_fb"], ["first" + s], scale=37.0, bias=T.cols[:, 1:2])
+                act(fs, T.pz[:, l0:l1], F.Relu, ["pz:" + s, "c_fb"], ["first" + s], scale=FIRST, bias=T.cols[:, 1:2])
                 yield
                 mm(u, T.blku[:], fs, False, True, ["blku", "first" + s], un)
                 yield
                 h = "A" if l0 < CUT else "B"
-                mm(T["pq" + h][:, 17 * q0:17 * q1], T.blkd[:], T.first[:, q0:q1, :], False, q1 == part[h][1],
-                   ["blkd", "first" + s, "first_0"], ["pq" + h])
+                mm(T["pq" + h][:, 17 * q0:17 * q1], T.blk37[:], T.first[:, q0:q1, :], False, q1 == part[h][1],
+                   ["blk37", "first" + s, "first_0"], ["pq" + h])
             elif w == "dh":
-                if passes_on and s in DH_SCALAR:
+                if not (passes_on or STEP_SCALAR):
+                    pass
+                elif s in DH_SCALAR:
                     act(T.dh[:, l0:l1], d, F.Identity, dn, ["dh" + s], bias=-2989.0)
-                elif passes_on:
+                else:
                     ts(T.dh[:, l0:l1], d, -2989.0, A.add, dn, ["dh" + s])
-            elif w == "xi":
+            elif w == "n":
+                act(T.nb[:, l0:l1], d, F.Identity, dn, ["nb" + s], scale=37.0 / 2048, bias=111.5 + 1.0 / 4096)
+                yield
+                e, en = T["pd" + s][:, L + l0:L + l1], ["pd%s:e" % s]
+                mm(e, T.blk[:], T.cd[:, l0:l1], True, False, ["blk", "cd"], en)
+                mm(e, T.eye37[:], T.dh[:, l0:l1], False, False, ["eye37", "dh" + s], en)
+                mm(e, T.eyen[:], T.nb[:, l0:l1], False, True, ["eyen", "nb" + s], en)
+            elif w == "xi" and s not in STEP_SCALAR:
                 tt(T.xi[:, l0:l1], d, fs, A.mult, dn + ["first" + s], ["xi" + s])
+            elif w == "xi":
+                tt(T.ei[:, l0:l1], T["pd" + s][:, L + l0:L + l1], fs, A.mult, ["pd%s:e" % s, "first" + s], ["ei" + s])
 
         def far(j):
             n = min(16 * j, CUT)
@@ -385,22 +405,26 @@ def rank_program(g, core, T, topo):
                ["pr:" + s for s in stages(CUT, 16 * j)] + ["kx"], ["hit%d" % j])
 
         def counted(s):
-            q0, q1 = part[s]
+            q0, q1 = WRITES[s]
             ts(T.ti[:, q0:q1], T.tsum[:, q0:q1], 512.0, A.mult, ["ts%d" % j for j in range(q0, q1)], ["ti" + s])
             yield
             ts(T.zi[:, q0:q1], T.ti[:, q0:q1], 511, A.bitwise_and, ["ti" + s], ["zi" + s])
             yield
-            tt(T.capA[:, 0::17] if s == "A" else T.capB[:, :, 0], T.zi[:, q0:q1], T.inbox[:, slot, q0:q1], A.add, ["zi" + s, kn], ["cap" + s])
+            tt(T.capB[:, :, 0] if s == "B" else T.capA[:, 17 * q0:17 * q1:17], T.zi[:, q0:q1], T.inbox[:, slot, q0:q1],
+               A.add, ["zi" + s, kn], ["cap" + s])
 
-        def winners(s):
+        def hits(s):
             q0, q1 = part[s]
             hit = T.hitA[:] if s == "A" else T.hitB[:, :, 0:17]
             ts(hit, T["pq" + s][:, 17 * q0:17 * q1], 0.0, A.is_equal, ["pq" + s], ["hit" + s])
-            yield
-            if s == "A":
-                op("v", lambda: v.tensor_tensor_scan(T.endA[:], T.hitA[:], T.capA[:], 0.0, A.add, A.min),
-                   ["hitA", "capA"], ["endA"])
-                end, en = T.endA[:, 16::17], ["endA"]
+
+        def winners(s):
+            q0, q1 = WRITES[s]
+            if s != "B":
+                c = slice(17 * q0, 17 * q1)
+                op("v", lambda: v.tensor_tensor_scan(T.endA[:, c], T.hitA[:, c], T.capA[:, c], 0.0, A.add, A.min),
+                   ["hitA", "cap" + s], ["end" + s])
+                end, en = T.endA[:, 17 * q0 + 16:17 * q1:17], ["end" + s]
             else:
                 for j in range(q1 - q0):
                     n = 17 + 16 * j
@@ -413,13 +437,15 @@ def rank_program(g, core, T, topo):
 
         def mend(s):
             l0, l1 = MENDS[s]
-            ts(T.ei[:, l0:l1], T.xi[:, l0:l1], 2047, A.bitwise_and, ["xi" + x for x in stages(l0, l1)], ["ei" + s])
-            yield
+            if not STEP_SCALAR:
+                ts(T.ei[:, l0:l1], T.xi[:, l0:l1], 2047, A.bitwise_and, ["xi" + x for x in stages(l0, l1)],
+                   ["ei" + x for x in stages(l0, l1)])
+                yield
             if plain:
                 base, rd = table.indirect(T.lu[:, c0 + l0 // 16:c0 + l1 // 16]), [luk]
             else:
                 base, rd = T.tab[:, 0:2 * V].indirect(T.lu[:, c0 + 16 + l0 // 16:c0 + 16 + l1 // 16]), ["ch0", lum]
-            tt(T.si[:, l0:l1], base, T.ei[:, l0:l1], A.add, rd + ["ei" + s, "tab" + s, "tab"], ["si" + s])
+            tt(T.si[:, l0:l1], base, T.ei[:, l0:l1], A.add, rd + ["tab"] + ["ei" + x for x in stages(l0, l1)], ["si" + s])
             yield
             ts(T.col[:, l0:l1], T.si[:, l0:l1], R - 1, A.bitwise_and, ["si" + s], ["col" + s])
 
@@ -441,7 +467,7 @@ def rank_program(g, core, T, topo):
 
         def new_marks():
             if passes_on:
-                ts(T.lost[:], T.ou[:], 2048.0, A.is_ge, ["ouA", "ouB"], ["lost"], 0.5, A.mult)
+                ts(T.lost[:], T.ou[:], 2048.0, A.is_ge, ["ou" + s for s in WRITES], ["lost"], 0.5, A.mult)
                 yield
                 tt(T.nm[:], T.lost[:], T.um[:], A.min, ["lost", "um"], ["nm"])
                 yield
@@ -455,10 +481,13 @@ def rank_program(g, core, T, topo):
             elif w in ("M", "K", "nm"):
                 yield from {"M": marks, "K": keys, "nm": new_marks}[w]()
             elif w[0] == "W":
-                q0, q1 = part[w[1]]
-                cp(table.indirect(T.ou[:, q0:q1]), T.col[:, 16 * q0:16 * q1], ["ou" + w[1], "col" + w[1]],
+                q0, q1 = WRITES[w[1]]
+                cp(table.indirect(T.ou[:, q0:q1]), T.col[:, 16 * q0:16 * q1],
+                   ["ou" + w[1]] + ["col" + s for s, (l0, l1) in MENDS.items() if l0 < 16 * q1 and l1 > 16 * q0],
                    ["tab" + w[1], "tab"])
-            elif w[-1] in "AB":
+            elif w[0] == "h":
+                hits(w[1])
+            elif w[-1] in "ABCD":
                 yield from {"q": near, "z": counted, "o": winners, "m": mend}[w[0]](w[1])
             elif "." in w:
                 yield from staged(*w.split("."))
@@ -470,8 +499,10 @@ def rank_program(g, core, T, topo):
             if w not in live:
                 live[w] = step(w)
             next(live[w], None)
+        if t == 0 and r > 0:
+            act(T.tab[:, 0:V], T.chi[:], F.Copy, ["chi"], ["ch0"])
 
-    dma("s", "st_c", T.yc[:], T.tab[:, V:2 * V], ["tabA", "tabB"], [])
+    dma("s", "st_c", T.yc[:], T.tab[:, V:2 * V], tabs, [])
     tt(T.lost[:], T.outbox[:, ROUNDS - 1, 0:16], T.nm[:], A.subtract, ["out%dk" % (ROUNDS - 1), "nm"], ["lost"])
     ts(T.vh[:], T.lost[:], 0.5, A.add, ["lost"], ["vh"])
     rows(T.vh[:], "vh")

from concourse.mybir import AluOpType as A, ActivationFunctionType as F

V, R, L, ROUNDS, N = 2048, 4096, 256, 8, 4
CUT = 192
PIECES = ((0, 64, "P"), (64, 128, "R"), (128, 192, "P"), (192, 256, "Q"))
SUMS = ((0, 64), (64, 128), (128, 192), (192, 256))
CANDS = ((0, 128), (128, 256))
STAGES = {"a": (0, 128), "b": (128, 192), "c": (192, 256)}
MENDS = {"A": (0, 128), "C": (128, 192), "B": (192, 256)}
WRITES = {"A": (0, 8), "C": (8, 12), "B": (12, 16)}
DH_SCALAR = "c"
STEP_SCALAR = ""
FIRST = 1.0 if STEP_SCALAR else 37.0
ORDER = ("c0 qB g1 c1 g0 i.a g2 qA M l1 b0 b1 s0 g3 b3 b2 M kx s1 i.c sg.a i.b s2 sg.a tb M sg.b u.a fi.a qA xi.a sg.b "
         "dh.a fi.b dh.b kmu fi.a u.b mA xi.b mA l3 r1 s3 r2 r3 u.c fi.a r7 r4 r6 r5 zA dh.c fi.b sg.c qB r8 r9 fi.b "
         "mA sg.c fi.c fi.c fi.c zA r11 mC hA zA mC xi.c r10 oA r15 hB e14 r12 zC oA r13 mC K mB zC WA r14 zC K zB e15 "
         "K zB oC K e13 zB mB oC oB WC oB mB nm um WB nm ku nm")
HALVES = 1.5 * 2 ** 22
WIDE = 1 + L - CUT

SCRATCH = {n: ("sbuf", s, d) for d, s, names in (
    ("bfloat16", [128, R], "recs ax0 ax1 ax2 ax3 diff absd"),
    ("bfloat16", [128, L], "atom sgn nb cd zero ones"),
    ("bfloat16", [128, 16, 17], "first mrow"),
    ("bfloat16", [128, 16, L], "junk"),
    ("bfloat16", [128, 128], "c1 c2 c3 blk eye eyem eyeu eye37 eyen low blku blkd blk37 xm"),
    ("bfloat16", [128, 144], "slide sliden slidew"),
    ("bfloat16", [128, 16, 128], "sel seld"),
    ("bfloat16", [128, 272], "ownr m1"),
    ("bfloat16", [128, CUT // 16 * 17], "hitA"),
    ("bfloat16", [128, (L - CUT) // 16, WIDE], "hitB"),
    ("float16", [128, 128], "eyed eyeh maskt"),
    ("float16", [128, ROUNDS, 32], "inbox outbox"),
    ("float16", [128, L], "dh vrow"),
    ("float16", [128, 16], "vh"),
    ("uint16", [128, ROUNDS * 32], "lu"),
    ("uint16", [128, L], "cand"),
    ("uint16", [128, 16], "ou"),
    ("int32", [128, V], "chi"),
    ("int32", [128, L], "xi ei si col"),
    ("int32", [128, 16], "k0i ti zi"),
    ("int32", [128, 4], "thi wi pi pj"),
    ("float32", [128, 2 * V + L + 8], "tab"),
    ("float32", [128, L], "krow"),
    ("float32", [128, CUT // 16 * 17], "capA endA"),
    ("float32", [128, (L - CUT) // 16, WIDE], "capB endB"),
    ("float32", [128, 128], "c4 c5"),
    ("float32", [128, 16], "tsum tb kx um lost nm i16 own lo hi k1 k2"),
    ("float32", [128, 8], "cols"),
) for n in names.split()}
BANKS = ("pda", "pdb", "pdc", "pz", "pu", "pr", "pqA", "pqB")
SCRATCH.update({n: ("psum", [128, 512], "float32") for n in BANKS})
SEMAPHORES = (["v", "a", "p", "gp", "l_at", "l_k0", "l_th", "l_w", "l_ch", "l_rec", "sent", "st_c", "st_k"]
              + ["%s%d" % (x, t) for x in ("key", "mark") for t in range(1, ROUNDS)]
              + ["tile%d" % k for k in range(1, N)])


def rank_program(g, core, T, topo):
    r = T.rank_of(core)
    if r is None:
        return
    queue = {"v": g.vector, "a": g.scalar, "p": g.tensor, "gp": g, "s": g.sync}
    count = {"v": 0, "a": 0, "p": 0, "gp": 0}
    known = {e: {} for e in queue}
    clock = {}
    writer, readers, bank = {}, {}, {b: {} for b in BANKS}

    def wait(e, deps):
        need = {}
        for s, n in deps:
            need[s] = max(need.get(s, 0), n)
        todo = [(s, n) for s, n in need.items() if known[e].get(s, 0) < n]
        for s, n in todo:
            if any(clock.get(o, {}).get(s, 0) >= n for o in todo if o != (s, n)):
                continue
            queue[e].wait_ge(T.sem[s], n)
        for s, n in todo:
            known[e][s] = max(known[e].get(s, 0), n)
            for s2, n2 in clock.get((s, n), {}).items():
                known[e][s2] = max(known[e].get(s2, 0), n2)

    def deps_of(e, rd, wr):
        deps = [writer[x] for x in rd if x in writer]
        for x in wr:
            if x in writer:
                deps.append(writer[x])
            deps += readers.get(x, [])
        for x in list(rd) + list(wr):
            b = x.split(":")[0]
            if b in bank:
                deps += [(o, n) for o, n in bank[b].items() if o != e]
        if e == "p":
            deps = [d for d in deps if d[0] != "p"]
        return deps

    def note(tag, rd, wr):
        for x in rd:
            readers.setdefault(x, []).append(tag)
        for x in wr:
            writer[x] = tag
            readers[x] = []

    def op(e, call, rd, wr):
        wait(e, deps_of(e, rd, wr))
        call().then_inc(T.sem[e], 1)
        count[e] += 1
        tag = (e, count[e])
        clock[tag] = dict(known[e])
        note(tag, rd, wr)
        for x in list(rd) + list(wr):
            b = x.split(":")[0]
            if b in bank:
                bank[b][e] = count[e]

    def dma(e, sem, out, in_, rd, wr):
        wait(e, deps_of(e, rd, wr))
        queue[e].dma_start(out, in_).then_inc(T.sem[sem], 16)
        clock[(sem, 16)] = dict(known[e])
        note((sem, 16), rd, wr)

    sent = [0]

    def send(to, out, in_, sems, small, rd):
        dst = T.cores[to]
        eng = topo.engines(core, dst)
        half = len(eng) // 2
        use = eng[:half] if small else eng[half:]
        rid, pid = topo.addr(dst)[:2]
        wait("gp", deps_of("gp", rd, []))
        g.remote_dma(out, in_, T.sem[sems], T.sem.sent, pid, rid, sum(1 << x for x in use))
        sent[0] += len(use)

    def arrives(name, sem, frm):
        writer[name] = (sem, len(topo.engines(T.cores[frm], core)) // 2)

    v, a, p = g.vector, g.scalar, g.tensor

    def ts(out, in0, s1, op0, rd, wr, s2=None, op1=None):
        if op1 is None:
            op("v", lambda: v.tensor_scalar(out, in0, s1, None, op0), rd, wr)
        else:
            op("v", lambda: v.tensor_scalar(out, in0, s1, s2, op0, op1), rd, wr)

    def tt(out, in0, in1, o, rd, wr):
        op("v", lambda: v.tensor_tensor(out, in0, in1, o), rd, wr)

    def cp(out, in_, rd, wr):
        op("v", lambda: v.tensor_copy(out, in_), rd, wr)

    def fill(ap, c, wr):
        op("v", lambda: v.memset(ap, c), [], wr)

    def act(out, in_, f, rd, wr, **kw):
        op("a", lambda: a.activation(out, in_, f, **kw), rd, wr)

    def mm(out, lhs, rhs, start, stop, rd, wr):
        op("p", lambda: p.matmul(out, lhs, rhs, start, stop), rd, wr)

    def gp(call, rd, wr):
        op("gp", call, rd, wr)

    dma("s", "l_at", T.atom[:], T.at[:], [], ["atom"])
    dma("a", "l_k0", T.k0i[:], T.key0[:], [], ["k0i"])
    dma("s", "l_th", T.thi[:, 0:1], T.th[:], [], ["thi"])
    dma("a", "l_w", T.wi[:, 0:1], T.w[:], [], ["wi"])
    dma("s", "l_ch", T.chi[:], T.ch[:], [], ["chi"])
    dma("s", "l_rec", T.recs[:], T.rec[:], [], ["recs"])
    for k in range(1, N):
        arrives("ax%d" % k, "tile%d" % k, (r - k) % N)
    for t in range(1, ROUNDS):
        if r > 0:
            arrives("key%d" % t, "key%d" % t, r - 1)
            arrives("mark%d" % t, "mark%d" % t, r - 1)
        elif t < N:
            arrives("key%d" % t, "key%d" % t, N - t)
            arrives("mark%d" % t, "key%d" % t, N - t)

    part = {"A": (0, CUT // 16), "B": (CUT // 16, 16)}
    fill(T.ones[:], 1.0, ["ones"])
    one = T.ones[:, 0:128]
    gp(lambda: g.iota(T.pi[:, 0:1], [[0, 1]], 0, 1), [], ["pi"])
    gp(lambda: g.iota(T.i16[:], [[1, 16]], 0, 0, allow_small_or_imprecise_dtypes=True), [], ["i16"])
    gp(lambda: g.affine_select(T.eye[:], one, [[-1, 128]], A.is_equal, 0.0, 0, 1), ["ones"], ["eye"])
    gp(lambda: g.affine_select(T.c1[:], one, [[-16, 8], [0, 16]], A.is_ge, 0.0, 0, 1), ["ones"], ["c1"])
    gp(lambda: g.affine_select(T.blk[:], T.c1[:], [[16, 8], [0, 16]], A.is_ge, 0.0, 15, -1), ["c1"], ["blk"])
    gp(lambda: g.affine_select(T.c3[:], T.blk[:], [[1, 128]], A.is_gt, 0.0, 0, -1), ["blk"], ["c3"])
    gp(lambda: g.iota(T.m1[:], [[0, 16], [1, 17]], -1, 0, allow_small_or_imprecise_dtypes=True), [], ["m1"])
    for s, (q0, q1) in part.items():
        gp(lambda: g.iota(T["end" + s][:], [[16, q1 - q0], [0, 17 if s == "A" else WIDE]], 16 * q0 + 1, 0,
                          allow_small_or_imprecise_dtypes=True), [], ["end" + s])
    act(T.tsum[:], T.ones[:, 0:16], F.Tanh, ["ones"], ["ts%d" % j for j in range(16)], scale=0.0)
    fill(T.junk[:, :, 0:128], float(R), ["junk%d" % j for j in range(16)])
    fill(T.slide[:], 0.0, ["slide"])
    fill(T.zero[:], 0.0, ["zero"])
    fill(T.first[:, :, 0], 0.0, ["first_0"])
    fill(T.mrow[:, :, 0], 0.0, ["mrow_0"])
    fill(T.tab[:, 2 * V:], 0.0, ["spare"])
    ts(T.pj[:, 0:1], T.pi[:, 0:1], 15, A.bitwise_and, ["pi"], ["pj"])
    cp(T.cols[:, 0:1], T.pj[:, 0:1], ["pj"], ["c_pl"])
    ts(T.cols[:, 1:2], T.pj[:, 0:1], -FIRST, A.mult, ["pj"], ["c_fb"], -18.5 * FIRST, A.add)
    ts(T.own[:], T.i16[:], T.cols[:, 0:1], A.is_equal, ["i16", "c_pl"], ["own"])
    ts(T.hi[:], T.own[:], 64.0, A.mult, ["own"], ["hi"])
    ts(T.lo[:], T.own[:], -1.0, A.add, ["own"], ["lo"], 64.0, A.mult)
    ts(T.inbox[:, 0, 0:16], T.k0i[:], -2048.0, A.add, ["k0i"], ["key0"], 1.0 / R, A.mult)
    ts(T.inbox[:, 0, 16:32], T.k0i[:], 1.0 / R, A.mult, ["k0i"], ["mark0"])
    if r > 0:
        send(0, T.inbox[:, N - r, :], T.inbox[:, 0, :], "key%d" % (N - r), True, ["key0", "mark0"])
    gp(lambda: g.affine_select(T.sel[:], T.junk[:, :, 0:128], [[-1, 16], [-16, 8], [0, 16]], A.is_equal, 0.0, 0, 1),
       ["junk%d" % j for j in range(16)], ["sel"])
    for name, src, c in (("c2", "eye", -2.0), ("eyem", "eye", 18.5), ("eyeu", "eye", 160.0),
                         ("eye37", "eye", 37.0), ("eyen", "eye", -2048.0), ("blku", "blk", -64.0 * 37 / FIRST),
                         ("blkd", "blk", -1.0), ("blk37", "blk", -37.0 / FIRST)):
        act(T[name][:], T[src][:], F.Identity, [src], [name], scale=c)
    tt(T.c1[:], T.blk[:], T.c2[:], A.add, ["blk", "c2"], ["c1"])
    tt(T.low[:], T.eye[:], T.c3[:], A.subtract, ["eye", "c3"], ["low"])
    ts(T.xm[:], T.c1[:], 64.0, A.mult, ["c1"], ["xm"])
    for i in range(16):
        if i < 10:
            cp(T.ax0[:, i::16], T.atom[:], ["atom"], ["ax0_%d" % i])
        else:
            act(T.ax0[:, i::16], T.atom[:], F.Copy, ["atom"], ["ax0_%d" % i])
    ax0 = ["ax0_%d" % i for i in range(16)]
    ts(T.slide[:, 15:143:16], T.blk[:, 0::16], 2.0, A.mult, ["blk", "slide"], ["slide"])
    act(T.sliden[:], T.slide[:], F.Identity, ["slide"], ["sliden"], scale=-0.5)
    ts(T.cols[:, 2:3], T.thi[:, 0:1], -1.0, A.mult, ["thi"], ["c_th"], -941.5, A.add)
    cp(T.cols[:, 3:4], T.wi[:, 0:1], ["wi"], ["c_w"])
    ts(T.eyed[:], T.eye[:], 941.0, A.mult, ["eye"], ["eyed"])
    ts(T.ownr[:], T.m1[:], T.cols[:, 0:1], A.is_equal, ["m1", "c_pl"], ["ownr"])
    ts(T.slidew[:], T.slide[:], T.cols[:, 3:4], A.mult, ["slide", "c_w"], ["slidew"], 0.5 / R, A.mult)
    ts(T.eyeh[:], T.eye[:], -1023.5 / R, A.mult, ["eye"], ["eyeh"])
    ts(T.cols[:, 5:6], T.own[:, 0:1], 166.0 * 2048, A.mult, ["own"], ["c_cd"], T.own[:, 1:2], A.add)
    act(T.cd[:], T.ones[:], F.Identity, ["ones", "c_cd"], ["cd"], scale=T.cols[:, 5:6])
    for s in part:
        ts(T["cap" + s][:], T["end" + s][:], T.cols[:, 0:1], A.add, ["endA", "endB", "endC", "endD", "c_pl"] + ["endB%d" % j for j in range(4)],
           ["cap" + x for x in WRITES if (x == "B") == (s == "B")], 1.0 / R, A.mult)
    act(T.c4[:], T.c1[:], F.Identity, ["c1"], ["c4"], scale=5 * 18.5)
    act(T.c5[:], T.low[:], F.Identity, ["low"], ["c5"], scale=4 * 18.5)
    tabs = ["tab" + s for s in WRITES]
    act(T.tab[:, V:2 * V], T.chi[:], F.Copy, ["chi", "spare"], ["tab"] + tabs)
    tt(T.maskt[:], T.c4[:], T.c5[:], A.add, ["c4", "c5"], ["maskt"])
    for il in range(16):
        ts(T.seld[:, il, :], T.xm[:], T.lo[:, il:il + 1], A.max, ["xm", "lo", "hi"], ["seld%d" % il],
           T.hi[:, il:il + 1], A.min)
    wait("gp", [writer["recs"]])
    for k in range(1, N):
        send((r + k) % N, T["ax%d" % k][:], T.ax0[:], "tile%d" % k, False, ax0)

    table = T.tab[:, V:2 * V + L + 8]

    def stages(l0, l1):
        return [s for s in STAGES if STAGES[s][0] < l1 and STAGES[s][1] > l0]

    def slot_of(t):
        return t if r > 0 else t % N

    def offsets(t):
        ts(T.lu[:, 32 * t:32 * t + 16], T.inbox[:, slot_of(t), 0:16], float(R), A.mult, ["key%d" % slot_of(t)],
           ["luk%d" % t], 2048.0, A.add)

    def rows(lst, name):
        mm(T.pr[:, 0:L], T.eye[:], T.zero[:], True, False, ["eye", "zero"], ["pr:r", "pr:open"])
        for il in range(16):
            mm(T.pr[:, il:L:16], T.sel[:, il, :], lst, False, il == 15, ["sel", name], ["pr:r", "pr:open"])

    offsets(0)
    for t in range(ROUNDS):
        last = t == ROUNDS - 1
        passes_on = last or r < N - 1
        slot = slot_of(t)
        kn, mn, luk, lum, on = "key%d" % slot, "mark%d" % slot, "luk%d" % t, "lum%d" % t, "out%d" % t
        kq, km = T.inbox[:, slot, 0:16], T.inbox[:, slot, 16:32]
        c0 = 32 * t
        ax, axn = T["ax%d" % (t % N)], (ax0 if t % N == 0 else ["ax%d" % (t % N)])
        plain = t == 0 or r == 0
        left = {}

        def cands(c):
            l0, l1 = CANDS[c]
            cp(T.cand[:, l0:l1], table.indirect(T.lu[:, c0 + l0 // 16:c0 + l1 // 16]), tabs + [luk],
               ["cand%d" % q for q in range(l0 // 16, l1 // 16)])

        def small(w):
            if w == "ku" and not last:
                offsets(t + 1)
            elif w == "kmu" and not plain:
                ts(T.lu[:, c0 + 16:c0 + 32], km, float(R), A.mult, [mn], [lum], 2048.0, A.add)
            elif w == "tb":
                act(T.tb[:], kq, F.Identity, [kn], ["tb"], scale=-8.0 * R, bias=1280 + 1.0 / 512)
            elif w == "kx":
                act(T.kx[:], kq, F.Identity, [kn], ["kx"], scale=float(R), bias=-160.0)
            elif w == "um" and passes_on:
                act(T.um[:], km, F.Relu, [mn], ["um"], scale=float(R), bias=0.5)

        def marks():
            rows(km, mn)
            yield
            act(T.mrow[:, :, 1:17], T.pr[:, 0:L], F.Sign, ["pr:r"], ["mrow"], bias=0.5)
            yield
            act(T.vrow[:], T.pr[:, 0:L], F.Copy, ["pr:r"], ["vrow"])

        def near(s):
            q0, q1 = part[s]
            pq, on = T["pq" + s], ["pq" + s]
            mm(pq[:, 17 * q0:17 * q1], T.maskt[:], T.ownr[:, 17 * q0:17 * q1], True, False, ["maskt", "ownr"], on)
            for il in range(16):
                mm(pq[:, 17 * q0 + 1 + il:17 * q1:17], T.seld[:, il, :], T.inbox[:, slot, q0:q1], False, False,
                   ["seld%d" % il, kn], on)
            yield
            mm(pq[:, 17 * q0:17 * q1], T.eyem[:], T.mrow[:, q0:q1], False, False, ["eyem", "mrow", "mrow_0"], on)

        def gather(c):
            l0, l1, mode = PIECES[c]
            out, x = T.diff[:, 16 * l0:16 * l1], T.recs[:].indirect(T.cand[:, l0:l1])
            cn = ["cand%d" % q for q in range(l0 // 16, l1 // 16)]
            if mode == "R":
                act(out, x, F.Copy, ["recs"] + cn, ["diff%d" % c])
            else:
                tt(out, x, ax[:, 16 * l0:16 * l1], A.subtract, ["recs"] + cn + axn, ["diff%d" % c])

        def absval(c):
            l0, l1, mode = PIECES[c]
            out, x = T.absd[:, 16 * l0:16 * l1], T.diff[:, 16 * l0:16 * l1]
            if mode == "R":
                tt(out, x, ax[:, 16 * l0:16 * l1], A.max, ["diff%d" % c] + axn, ["abs%d" % c])
            elif mode == "Q":
                ts(out, x, 0.0, A.max, ["diff%d" % c], ["abs%d" % c])
            else:
                act(out, x, F.Abs, ["diff%d" % c], ["abs%d" % c], scale=0.5)

        def pieces(b, modes):
            cs = [c for c in range(len(PIECES)) if SUMS[b][0] <= PIECES[c][0] < SUMS[b][1] and PIECES[c][2] in modes]
            return (cs, min(PIECES[c][0] for c in cs), max(PIECES[c][1] for c in cs)) if cs else ([], 0, 0)

        def linear(b):
            l0, l1 = SUMS[b]
            s = stages(l0, l1)[0]
            out, on = T["pd" + s], ["pd%s:%d" % (s, b)]
            rs, n0, n1 = pieces(b, "R")
            if rs:
                mm(out[:, n0:n1], T.blkd[:], ax[:, 16 * n0:16 * n1:16], False, False, ["blkd"] + axn, on)
            cs, n0, n1 = pieces(b, "QR")
            for i in range(16 if cs else 0):
                mm(out[:, n0:n1], T.sliden[:, 15 - i:143 - i], T.diff[:, 16 * n0 + i:16 * n1:16], False, False,
                   ["sliden"] + ["diff%d" % c for c in cs], on)

        def sums(b):
            l0, l1 = SUMS[b]
            s = stages(l0, l1)[0]
            left[s] -= l1 - l0
            for i in range(16):
                mm(T["pd" + s][:, l0:l1], T.slide[:, 15 - i:143 - i], T.absd[:, 16 * l0 + i:16 * l1:16], False,
                   i == 15 and left[s] == 0, ["slide"] + ["abs%d" % c for c in pieces(b, "PQR")[0]], ["pd%s:%d" % (s, b)])

        def staged(w, s):
            l0, l1 = STAGES[s]
            q0, q1 = l0 // 16, l1 // 16
            d, dn = T["pd" + s][:, l0:l1], ["pd%s:%d" % (s, b) for b in range(len(SUMS)) if l0 <= SUMS[b][0] < l1]
            fs, ms = T.first[:, q0:q1, 1:17], T.mrow[:, q0:q1, 1:17]
            u, un = (T.pu[:, l0:l1], ["pu:" + s, "pu:open"]) if l0 < CUT else (T.pr[:, L + l0:L + l1], ["pr:" + s, "pr:open"])
            if w == "i":
                left[s] = l1 - l0
                mm(d, T.eyed[:], T.ones[:, l0:l1], True, False, ["eyed", "ones"], dn + ["pd%s:e" % s])
            elif w == "sg":
                act(T.sgn[:, l0:l1], d, F.Sign, dn + ["c_th"], ["sgn" + s], bias=T.cols[:, 2:3])
                yield
                mm(T.pz[:, l0:l1], T.eyem[:], ms, True, False, ["eyem", "mrow"], ["pz:" + s])
                mm(T.pz[:, l0:l1], T.low[:], T.sgn[:, l0:l1], False, True, ["low", "sgn" + s], ["pz:" + s])
            elif w == "u":
                mm(u, T.eye[:], T.vrow[:, l0:l1], True, False, ["eye", "vrow"], un)
                mm(u, T.eyeu[:], ms, False, False, ["eyeu", "mrow"], un)
            elif w == "fi":
                act(fs, T.pz[:, l0:l1], F.Relu, ["pz:" + s, "c_fb"], ["first" + s], scale=FIRST, bias=T.cols[:, 1:2])
                yield
                mm(u, T.blku[:], fs, False, True, ["blku", "first" + s], un)
                yield
                h = "A" if l0 < CUT else "B"
                mm(T["pq" + h][:, 17 * q0:17 * q1], T.blk37[:], T.first[:, q0:q1, :], False, q1 == part[h][1],
                   ["blk37", "first" + s, "first_0"], ["pq" + h])
            elif w == "dh":
                if not (passes_on or STEP_SCALAR):
                    pass
                elif s in DH_SCALAR:
                    act(T.dh[:, l0:l1], d, F.Identity, dn, ["dh" + s], bias=-2989.0)
                else:
                    ts(T.dh[:, l0:l1], d, -2989.0, A.add, dn, ["dh" + s])
            elif w == "n":
                act(T.nb[:, l0:l1], d, F.Identity, dn, ["nb" + s], scale=37.0 / 2048, bias=111.5 + 1.0 / 4096)
                yield
                e, en = T["pd" + s][:, L + l0:L + l1], ["pd%s:e" % s]
                mm(e, T.blk[:], T.cd[:, l0:l1], True, False, ["blk", "cd"], en)
                mm(e, T.eye37[:], T.dh[:, l0:l1], False, False, ["eye37", "dh" + s], en)
                mm(e, T.eyen[:], T.nb[:, l0:l1], False, True, ["eyen", "nb" + s], en)
            elif w == "xi" and s not in STEP_SCALAR:
                tt(T.xi[:, l0:l1], d, fs, A.mult, dn + ["first" + s], ["xi" + s])
            elif w == "xi":
                tt(T.ei[:, l0:l1], T["pd" + s][:, L + l0:L + l1], fs, A.mult, ["pd%s:e" % s, "first" + s], ["ei" + s])

        def far(j):
            n = min(16 * j, CUT)
            act(T.junk[:, j, 0:n], T.pu[:, 0:n], F.Tanh, ["pu:" + s for s in stages(0, n)] + ["tb"],
                ["junk%d" % j, "ts%d" % j], scale=8.0, bias=T.tb[:, j:j + 1], accum_out=T.tsum[:, j:j + 1])

        def late(j):
            ts(T.hitB[:, j - CUT // 16, 17:17 + 16 * j - CUT], T.pr[:, L + CUT:L + 16 * j], T.kx[:, j:j + 1], A.is_equal,
               ["pr:" + s for s in stages(CUT, 16 * j)] + ["kx"], ["hit%d" % j])

        def counted(s):
            q0, q1 = WRITES[s]
            ts(T.ti[:, q0:q1], T.tsum[:, q0:q1], 512.0, A.mult, ["ts%d" % j for j in range(q0, q1)], ["ti" + s])
            yield
            ts(T.zi[:, q0:q1], T.ti[:, q0:q1], 511, A.bitwise_and, ["ti" + s], ["zi" + s])
            yield
            tt(T.capB[:, :, 0] if s == "B" else T.capA[:, 17 * q0:17 * q1:17], T.zi[:, q0:q1], T.inbox[:, slot, q0:q1],
               A.add, ["zi" + s, kn], ["cap" + s])

        def hits(s):
            q0, q1 = part[s]
            hit = T.hitA[:] if s == "A" else T.hitB[:, :, 0:17]
            ts(hit, T["pq" + s][:, 17 * q0:17 * q1], 0.0, A.is_equal, ["pq" + s], ["hit" + s])

        def winners(s):
            q0, q1 = WRITES[s]
            if s != "B":
                c = slice(17 * q0, 17 * q1)
                op("v", lambda: v.tensor_tensor_scan(T.endA[:, c], T.hitA[:, c], T.capA[:, c], 0.0, A.add, A.min),
                   ["hitA", "cap" + s], ["end" + s])
                end, en = T.endA[:, 17 * q0 + 16:17 * q1:17], ["end" + s]
            else:
                for j in range(q1 - q0):
                    n = 17 + 16 * j
                    op("v", lambda: v.tensor_tensor_scan(T.endB[:, j, WIDE - n:WIDE], T.hitB[:, j, 0:n], T.capB[:, j, 0:n],
                                                         0.0, A.add, A.min),
                       ["hitB", "capB", "hit%d" % (q0 + j)], ["endB%d" % j])
                end, en = T.endB[:, :, WIDE - 1], ["endB%d" % j for j in range(q1 - q0)]
            yield
            ts(T.ou[:, q0:q1], end, float(R), A.mult, en, ["ou" + s], 2048.0, A.add)

        def mend(s):
            l0, l1 = MENDS[s]
            if not STEP_SCALAR:
                ts(T.ei[:, l0:l1], T.xi[:, l0:l1], 2047, A.bitwise_and, ["xi" + x for x in stages(l0, l1)],
                   ["ei" + x for x in stages(l0, l1)])
                yield
            if plain:
                base, rd = table.indirect(T.lu[:, c0 + l0 // 16:c0 + l1 // 16]), [luk]
            else:
                base, rd = T.tab[:, 0:2 * V].indirect(T.lu[:, c0 + 16 + l0 // 16:c0 + 16 + l1 // 16]), ["ch0", lum]
            tt(T.si[:, l0:l1], base, T.ei[:, l0:l1], A.add, rd + ["tab"] + ["ei" + x for x in stages(l0, l1)], ["si" + s])
            yield
            ts(T.col[:, l0:l1], T.si[:, l0:l1], R - 1, A.bitwise_and, ["si" + s], ["col" + s])

        def keys():
            if passes_on:
                o = T.pz[:, L:L + 16]
                mm(o, T.eyeh[:], T.ones[:, 0:16], True, False, ["eyeh", "ones"], ["pz:k"])
                for jl in range(16):
                    mm(o, T.slidew[:, 15 - jl:143 - jl], T.dh[:, jl::16], False, jl == 15,
                       ["slidew"] + ["dh" + s for s in STAGES], ["pz:k"])
                yield
                act(T.k1[:], o, F.Identity, ["pz:k"], ["k1"], bias=HALVES)
                yield
                ts(T.k2[:], T.k1[:], -HALVES, A.add, ["k1"], ["k2"], 1024.5 / R, A.add)
                yield
                tt(T.outbox[:, t, 0:16], o, T.k2[:], A.subtract, ["pz:k", "k2"], [on + "k"])
                if not last:
                    send(r + 1, T.inbox[:, t + 1, 0:16], T.outbox[:, t, 0:16], "key%d" % (t + 1), True, [on + "k"])

        def new_marks():
            if passes_on:
                ts(T.lost[:], T.ou[:], 2048.0, A.is_ge, ["ou" + s for s in WRITES], ["lost"], 0.5, A.mult)
                yield
                tt(T.nm[:], T.lost[:], T.um[:], A.min, ["lost", "um"], ["nm"])
                yield
                if not last:
                    tt(T.outbox[:, t, 16:32], T.nm[:], T.outbox[:, t, 0:16], A.add, ["nm", on + "k"], [on + "m"])
                    send(r + 1, T.inbox[:, t + 1, 16:32], T.outbox[:, t, 16:32], "mark%d" % (t + 1), True, [on + "m"])

        def step(w):
            if w in ("ku", "kmu", "tb", "kx", "um"):
                small(w)
            elif w in ("M", "K", "nm"):
                yield from {"M": marks, "K": keys, "nm": new_marks}[w]()
            elif w[0] == "W":
                q0, q1 = WRITES[w[1]]
                cp(table.indirect(T.ou[:, q0:q1]), T.col[:, 16 * q0:16 * q1],
                   ["ou" + w[1]] + ["col" + s for s, (l0, l1) in MENDS.items() if l0 < 16 * q1 and l1 > 16 * q0],
                   ["tab" + w[1], "tab"])
            elif w[0] == "h":
                hits(w[1])
            elif w[-1] in "ABCD":
                yield from {"q": near, "z": counted, "o": winners, "m": mend}[w[0]](w[1])
            elif "." in w:
                yield from staged(*w.split("."))
            else:
                {"c": cands, "g": gather, "b": absval, "l": linear, "s": sums, "r": far, "e": late}[w[0]](int(w[1:]))

        live = {}
        for w in ORDER.split():
            if w not in live:
                live[w] = step(w)
            next(live[w], None)
        if t == 0 and r > 0:
            act(T.tab[:, 0:V], T.chi[:], F.Copy, ["chi"], ["ch0"])

    dma("s", "st_c", T.yc[:], T.tab[:, V:2 * V], tabs, [])
    tt(T.lost[:], T.outbox[:, ROUNDS - 1, 0:16], T.nm[:], A.subtract, ["out%dk" % (ROUNDS - 1), "nm"], ["lost"])
    ts(T.vh[:], T.lost[:], 0.5, A.add, ["lost"], ["vh"])
    rows(T.vh[:], "vh")
    act(T.krow[:], T.pr[:, 0:L], F.Identity, ["pr:r"], ["krow"], bias=2048.0)
    dma("a", "st_k", T.yk[:], T.krow[0:128:16, :], ["krow"], [])
    g.wait_ge(T.sem.sent, sent[0])
    wait("gp", [(e, n) for e, n in count.items()] + [("st_c", 16), ("st_k", 16)])
